import numpy as np
import ml_dtypes


def mxq(x, axis, fmt="e4m3"):
    dtype, down = {"e4m3": (ml_dtypes.float8_e4m3fn, 7), "e5m2": (ml_dtypes.float8_e5m2, 14)}[fmt]
    v = np.moveaxis(np.asarray(x, np.float32).astype(ml_dtypes.bfloat16).astype(np.float64), axis, -1)
    blocks = v.reshape(v.shape[:-1] + (-1, 32))
    amax = np.abs(blocks).max(-1, keepdims=True)
    byte = np.maximum(np.where(amax > 0, np.frexp(amax)[1] - 1 + 127, 0) - down, 1)
    scale = np.exp2(byte - 127.0)
    codes = (blocks / scale).astype(np.float32).astype(dtype).astype(np.float64)
    return np.moveaxis((codes * scale).reshape(v.shape), -1, axis)


WIDE = False


def mx_kscale(k):
    if not WIDE:
        return np.ones(k)
    levels = np.array([18, -18])
    if k % 512:
        return np.exp2(np.random.permutation(np.resize(levels, k // 32))).repeat(32)
    a = np.empty((k // 512, 16))
    for p in range(k // 512):
        a[p, :8] = np.random.permutation(np.resize(levels, 8))
        for g in range(8):
            far = levels[np.abs(levels - a[p, g]) >= 10]
            a[p, g + 8] = far[np.random.randint(len(far))]
    return np.exp2(a.ravel()).repeat(32)


def f64(x):
    return np.asarray(x).astype(np.float64)


def striped(idx):
    return np.tile(np.asarray(idx).reshape(-1, 16).T, (8, 1)).astype(np.uint16)


def unstriped(offs):
    return offs[:16].T.reshape(-1).astype(np.int64)


B, N, T, D, R = 1, 512, 2048, 512, 512


def setup_inputs():
    n = np.random.standard_normal
    idx = np.random.permutation(T)[:B * N]
    s = mx_kscale(D)[:, None]
    z = mx_kscale(R)[:, None]
    x = n((B, D, R))
    return {
        "xT": (x * s).astype(np.float32),
        "wT": (n((D, T)) * (1.00 / np.sqrt(D)) / s).astype(np.float32),
        "vT": (n((D, T)) / np.sqrt(D) / s).astype(np.float32),
        "wt": (np.random.uniform(0.5, 1.5, (B, R, 1)) * 1.0 / np.sqrt(R) * z).astype(np.float32),
        "xm": (x.transpose(0, 2, 1) / z).astype(np.float32),
        "offs": striped(idx),
    }


def reference(xT, wT, vT, wt, xm, offs):
    idx = unstriped(offs)
    pick = lambda x: x[:, idx].reshape(x.shape[0], B, N).transpose(1, 0, 2)
    xq = mxq(f64(xT), 1, "e4m3").transpose(0, 2, 1)
    a = xq @ mxq(pick(f64(wT)), 1, "e4m3")
    av = xq @ mxq(pick(f64(vT)), 1, "e4m3")
    g = f64(wt) * np.tanh(a - av)
    dw = mxq(f64(xm), 1, "e4m3").transpose(0, 2, 1) @ mxq(g, 1, "e5m2")
    gw = np.zeros((D, T))
    gw[:, idx] = dw.transpose(1, 0, 2).reshape(D, B * N)
    return gw

@@ -1,0 +1,179 @@
+from contextlib import ExitStack
+
+import concourse.mybir as mybir
+
+N, T, D, R = 512, 2048, 512, 512
+FLOPS = 3 * 2 * R * D * N
+
+F32 = mybir.dt.float32
+BF16 = mybir.dt.bfloat16
+U32 = mybir.dt.uint32
+U16 = mybir.dt.uint16
+U8 = mybir.dt.uint8
+E4M3 = mybir.dt.float8_e4m3fn_x4
+E5M2 = mybir.dt.float8_e5m2_x4
+ACT = mybir.ActivationFunctionType
+MULT = mybir.AluOpType.mult
+
+P = 128
+PACK = 4
+HALVES = 2
+HALF = N // HALVES
+LIST_COLS = HALF // 16
+
+
+def tile_attend_gds_lch_kernel(tc, xT, wT, vT, wt, xm, offs, out):
+    nc = tc.nc
+    with ExitStack() as ctx:
+        sb = ctx.enter_context(tc.tile_pool(name="sb", bufs=1))
+        psum = ctx.enter_context(tc.psum_pool(name="psum", bufs=1))
+
+        def mx_tiles(name, width):
+            codes = sb.tile([P, width], U32, name=name + "_codes", align_bytes=64)
+            scales = sb.tile([P, width], U8, name=name + "_scales", align_bytes=64)
+            return codes, scales
+
+        offsets = sb.tile([P, N // 16], U16, name="offsets")
+        nc.sync.dma_start(offsets[:], offs)
+        half_lists = [offsets[:, h * LIST_COLS : (h + 1) * LIST_COLS] for h in range(HALVES)]
+
+        row_weights = sb.tile([P, PACK], F32, name="row_weights")
+        nc.scalar.dma_start(row_weights[:], wt[0].rearrange("(p t) o -> p (t o)", t=PACK))
+
+        x_raw = sb.tile([P, PACK, R], F32, name="x_raw")
+        nc.sync.dma_start(x_raw[:], xT[0].rearrange("(p j) r -> p j r", j=PACK))
+        w_planes = [sb.tile([P, T], F32, name="w_plane%d" % j) for j in range(PACK)]
+        v_planes = [sb.tile([P, T], F32, name="v_plane%d" % j) for j in range(PACK)]
+        w_rows = wT.rearrange("(p j) c -> p j c", j=PACK)
+        v_rows = vT.rearrange("(p j) c -> p j c", j=PACK)
+        for j in range(PACK):
+            nc.sync.dma_start(w_planes[j][:], w_rows[:, j, :])
+        for j in range(PACK):
+            nc.sync.dma_start(v_planes[j][:], v_rows[:, j, :])
+        xm_raw = sb.tile([P, PACK, D], F32, name="xm_raw")
+        nc.sync.dma_start(xm_raw[:], xm[0].rearrange("(p t) d -> p t d", t=PACK))
+
+        warm = sb.tile([P, 1], F32, name="warm")
+        nc.scalar.activation(warm[:], row_weights[:, 0:1], ACT.Tanh)
+
+        windows = [sb.tile([P, T], F32, name="window%d" % u) for u in range(D // P)]
+        for window in windows:
+            nc.vector.memset(window[:], 0.0)
+
+        x_grouped = sb.tile([P, R * PACK], BF16, name="x_grouped", align_bytes=64)
+        nc.scalar.copy(
+            x_grouped[:].rearrange("p (t m j) -> p m j t", t=PACK, j=PACK),
+            x_raw[:].rearrange("p j (m t) -> p m j t", t=PACK),
+        )
+        x_codes, x_scales = mx_tiles("x", R)
+        nc.vector.quantize_mx(x_codes[:].bitcast(E4M3), x_scales[:], x_grouped[:])
+
+        w_picked = sb.tile([P, PACK, N], F32, name="w_picked")
+        for j in range(PACK):
+            nc.vector.tensor_copy(w_picked[:, j, :], w_planes[j][:].indirect(offsets[:]))
+        w_grouped = sb.tile([P, N * PACK], BF16, name="w_grouped", align_bytes=64)
+        nc.scalar.activation(
+            w_grouped[:].rearrange("p (c i j) -> p c j i", i=4, j=PACK),
+            w_picked[:].rearrange("p j (c i) -> p c j i", i=4),
+            ACT.Copy,
+            scale=-1.0,
+        )
+        w_codes, w_scales = mx_tiles("w", N)
+        nc.vector.quantize_mx(w_codes[:].bitcast(E4M3), w_scales[:], w_grouped[:])
+
+        scores = [
+            [psum.tile([P, HALF], F32, name="scores%d%d" % (h, t), tag="bank%d" % (h * PACK + t)) for t in range(PACK)]
+            for h in range(HALVES)
+        ]
+        for h in range(HALVES):
+            slots = slice(h * HALF, (h + 1) * HALF)
+            for t in range(PACK):
+                rows = slice(t * P, (t + 1) * P)
+                nc.tensor.matmul_mx(
+                    scores[h][t][:],
+                    lhsT=x_codes[:, rows].bitcast(E4M3),
+                    lhsT_scale=x_scales[:, rows],
+                    rhs=w_codes[:, slots].bitcast(E4M3),
+                    rhs_scale=w_scales[:, slots],
+                    start=True,
+                    stop=False,
+                )
+
+        v_grouped = [sb.tile([P, HALF, PACK], BF16, name="v_grouped%d" % h, align_bytes=64) for h in range(HALVES)]
+        v_mx = [mx_tiles("v%d" % h, HALF) for h in range(HALVES)]
+        slopes = [sb.tile([P, PACK, HALF], F32, name="slopes%d" % h) for h in range(HALVES)]
+        g_grouped = [sb.tile([P, HALF * PACK], BF16, name="g_grouped%d" % h, align_bytes=64) for h in range(HALVES)]
+        g_codes, g_scales = mx_tiles("g", N)
+        for j in range(PACK - 1):
+            for h in range(HALVES):
+                nc.vector.tensor_copy(v_grouped[h][:, :, j], v_planes[j][:].indirect(half_lists[h]))
+        for h in range(HALVES):
+            nc.vector.tensor_copy(v_grouped[h][:, :, PACK - 1], v_planes[PACK - 1][:].indirect(half_lists[h]))
+            v_codes, v_scales = v_mx[h]
+            nc.vector.quantize_mx(v_codes[:].bitcast(E4M3), v_scales[:], v_grouped[h][:].rearrange("p n j -> p (n j)"))
+            for t in range(PACK):
+                rows = slice(t * P, (t + 1) * P)
+                nc.tensor.matmul_mx(
+                    scores[h][t][:],
+                    lhsT=x_codes[:, rows].bitcast(E4M3),
+                    lhsT_scale=x_scales[:, rows],
+                    rhs=v_codes[:].bitcast(E4M3),
+                    rhs_scale=v_scales[:],
+                    start=False,
+                    stop=True,
+                )
+                nc.scalar.activation(slopes[h][:, t, :], scores[h][t][:], ACT.Tanh, scale=-1.0)
+
+        xm_grouped = [sb.tile([P, P * PACK], BF16, name="xm_grouped%d" % u, align_bytes=64) for u in range(D // P)]
+        xm_mx = [mx_tiles("xm%d" % u, P) for u in range(D // P)]
+
+        def group_xm(u):
+            nc.scalar.copy(
+                xm_grouped[u][:].rearrange("p (c i t) -> p c t i", i=4, t=PACK),
+                xm_raw[:, :, u * P : (u + 1) * P].rearrange("p t (c i) -> p c t i", i=4),
+            )
+
+        def quantize_xm(u):
+            nc.vector.quantize_mx(xm_mx[u][0][:].bitcast(E4M3), xm_mx[u][1][:], xm_grouped[u][:])
+
+        weights_wide = row_weights[:].unsqueeze(1).unsqueeze(3).to_broadcast([P, HALF // 4, PACK, 4])
+
+        def weigh(h):
+            nc.vector.tensor_tensor(
+                g_grouped[h][:].rearrange("p (c i t) -> p c t i", i=4, t=PACK),
+                slopes[h][:].rearrange("p t (c i) -> p c t i", i=4),
+                weights_wide,
+                MULT,
+            )
+
+        def quantize_g(h):
+            slots = slice(h * HALF, (h + 1) * HALF)
+            nc.vector.quantize_mx(g_codes[:, slots].bitcast(E5M2), g_scales[:, slots], g_grouped[h][:])
+
+        group_xm(0)
+        group_xm(1)
+        weigh(0)
+        quantize_g(0)
+        weigh(1)
+        quantize_xm(0)
+        quantize_g(1)
+        quantize_xm(1)
+
+        for u in range(D // P):
+            if u >= 2:
+                group_xm(u)
+                quantize_xm(u)
+            grads = psum.tile([P, N], F32, name="grads%d" % u, tag="bank%d" % u)
+            nc.tensor.matmul_mx(
+                grads[:],
+                lhsT=xm_mx[u][0][:].bitcast(E4M3),
+                lhsT_scale=xm_mx[u][1][:],
+                rhs=g_codes[:].bitcast(E5M2),
+                rhs_scale=g_scales[:],
+                start=True,
+                stop=True,
+            )
+            staged = sb.tile([P, N], F32, name="staged%d" % u)
+            nc.scalar.copy(staged[:], grads[:])
+            nc.vector.tensor_copy(windows[u][:].indirect(offsets[:]), staged[:])
+            nc.sync.dma_start(out[u * P : (u + 1) * P, :], windows[u][:])

@@ -20,6 +20,9 @@ PACK = 4
 HALVES = 2
 HALF = N // HALVES
 LIST_COLS = HALF // 16
+OVERLAP = 32
+PIECES = 4
+PIECE = N // PIECES
 
 
 def tile_attend_gds_lch_kernel(tc, xT, wT, vT, wt, xm, offs, out):
@@ -29,12 +32,11 @@ def tile_attend_gds_lch_kernel(tc, xT, wT, vT, wt, xm, offs, out):
         psum = ctx.enter_context(tc.psum_pool(name="psum", bufs=1))
 
         def mx_tiles(name, width):
-            codes = sb.tile([P, width], U32, name=name + "_codes", align_bytes=64)
+            codes = sb.tile([P, width], U32, name=name + "_codes", tag=name + "_codes", align_bytes=64)
             scales = sb.tile([P, width], U8, name=name + "_scales", align_bytes=64)
             return codes, scales
 
         offsets = sb.tile([P, N // 16], U16, name="offsets")
-        nc.sync.dma_start(offsets[:], offs)
         half_lists = [offsets[:, h * LIST_COLS : (h + 1) * LIST_COLS] for h in range(HALVES)]
 
         row_weights = sb.tile([P, PACK], F32, name="row_weights")
@@ -42,6 +44,7 @@ def tile_attend_gds_lch_kernel(tc, xT, wT, vT, wt, xm, offs, out):
 
         x_raw = sb.tile([P, PACK, R], F32, name="x_raw")
         nc.sync.dma_start(x_raw[:], xT[0].rearrange("(p j) r -> p j r", j=PACK))
+        nc.sync.dma_start(offsets[:], offs)
         w_planes = [sb.tile([P, T], F32, name="w_plane%d" % j) for j in range(PACK)]
         v_planes = [sb.tile([P, T], F32, name="v_plane%d" % j) for j in range(PACK)]
         w_rows = wT.rearrange("(p j) c -> p j c", j=PACK)
@@ -81,98 +84,119 @@ def tile_attend_gds_lch_kernel(tc, xT, wT, vT, wt, xm, offs, out):
         w_codes, w_scales = mx_tiles("w", N)
         nc.vector.quantize_mx(w_codes[:].bitcast(E4M3), w_scales[:], w_grouped[:])
 
-        scores = [
-            [psum.tile([P, HALF], F32, name="scores%d%d" % (h, t), tag="bank%d" % (h * PACK + t)) for t in range(PACK)]
-            for h in range(HALVES)
-        ]
-        for h in range(HALVES):
-            slots = slice(h * HALF, (h + 1) * HALF)
+        scores = [psum.tile([P, PACK, PIECE], F32, name="scores%d" % q) for q in range(PIECES)]
+
+        def score_passes(q, codes, scales, opens):
             for t in range(PACK):
                 rows = slice(t * P, (t + 1) * P)
                 nc.tensor.matmul_mx(
-                    scores[h][t][:],
+                    scores[q][:, t, :],
                     lhsT=x_codes[:, rows].bitcast(E4M3),
                     lhsT_scale=x_scales[:, rows],
-                    rhs=w_codes[:, slots].bitcast(E4M3),
-                    rhs_scale=w_scales[:, slots],
-                    start=True,
-                    stop=False,
+                    rhs=codes.bitcast(E4M3),
+                    rhs_scale=scales,
+                    start=(opens and t == 0),
+                    stop=(not opens and t == PACK - 1),
                 )
 
-        v_grouped = [sb.tile([P, HALF, PACK], BF16, name="v_grouped%d" % h, align_bytes=64) for h in range(HALVES)]
-        v_mx = [mx_tiles("v%d" % h, HALF) for h in range(HALVES)]
-        slopes = [sb.tile([P, PACK, HALF], F32, name="slopes%d" % h) for h in range(HALVES)]
-        g_grouped = [sb.tile([P, HALF * PACK], BF16, name="g_grouped%d" % h, align_bytes=64) for h in range(HALVES)]
-        g_codes, g_scales = mx_tiles("g", N)
-        for j in range(PACK - 1):
-            for h in range(HALVES):
-                nc.vector.tensor_copy(v_grouped[h][:, :, j], v_planes[j][:].indirect(half_lists[h]))
-        for h in range(HALVES):
-            nc.vector.tensor_copy(v_grouped[h][:, :, PACK - 1], v_planes[PACK - 1][:].indirect(half_lists[h]))
-            v_codes, v_scales = v_mx[h]
-            nc.vector.quantize_mx(v_codes[:].bitcast(E4M3), v_scales[:], v_grouped[h][:].rearrange("p n j -> p (n j)"))
-            for t in range(PACK):
-                rows = slice(t * P, (t + 1) * P)
-                nc.tensor.matmul_mx(
-                    scores[h][t][:],
-                    lhsT=x_codes[:, rows].bitcast(E4M3),
-                    lhsT_scale=x_scales[:, rows],
-                    rhs=v_codes[:].bitcast(E4M3),
-                    rhs_scale=v_scales[:],
-                    start=False,
-                    stop=True,
-                )
-                nc.scalar.activation(slopes[h][:, t, :], scores[h][t][:], ACT.Tanh, scale=-1.0)
+        for q in range(PIECES):
+            slots = slice(q * PIECE, (q + 1) * PIECE)
+            score_passes(q, w_codes[:, slots], w_scales[:, slots], True)
 
-        xm_grouped = [sb.tile([P, P * PACK], BF16, name="xm_grouped%d" % u, align_bytes=64) for u in range(D // P)]
+        v_grouped = sb.tile([P, N, PACK], BF16, name="v_grouped", align_bytes=64)
+        v_mx = [mx_tiles("v%d" % q, PIECE) for q in range(PIECES)]
+        slopes = [sb.tile([P, PIECE, PACK], F32, name="slopes%d" % q) for q in range(PIECES)]
+        g_grouped = [sb.tile([P, PIECE, PACK], BF16, name="g_grouped%d" % q, align_bytes=64) for q in range(PIECES)]
+        g_codes, g_scales = mx_tiles("g", HALF + N)
+        nc.vector.memset(g_codes[:, :HALF], 0)
+        nc.vector.memset(g_scales[:, :HALF], 127)
         xm_mx = [mx_tiles("xm%d" % u, P) for u in range(D // P)]
+        xm_grouped = []
 
         def group_xm(u):
             nc.scalar.copy(
-                xm_grouped[u][:].rearrange("p (c i t) -> p c t i", i=4, t=PACK),
+                xm_grouped[u].rearrange("p (c i t) -> p c t i", i=4, t=PACK),
                 xm_raw[:, :, u * P : (u + 1) * P].rearrange("p t (c i) -> p c t i", i=4),
             )
 
         def quantize_xm(u):
-            nc.vector.quantize_mx(xm_mx[u][0][:].bitcast(E4M3), xm_mx[u][1][:], xm_grouped[u][:])
+            nc.vector.quantize_mx(xm_mx[u][0][:].bitcast(E4M3), xm_mx[u][1][:], xm_grouped[u])
 
-        weights_wide = row_weights[:].unsqueeze(1).unsqueeze(3).to_broadcast([P, HALF // 4, PACK, 4])
+        for j in range(PACK - 1):
+            nc.vector.tensor_copy(v_grouped[:, :, j], v_planes[j][:].indirect(offsets[:]))
+        for h in range(HALVES):
+            first, end = max(0, h * HALF - OVERLAP), (h + 1) * HALF
+            nc.vector.tensor_copy(
+                v_grouped[:, first:end, PACK - 1], v_planes[PACK - 1][:].indirect(offsets[:, first // 16 : end // 16])
+            )
+            for q in range(h * PIECES // HALVES, (h + 1) * PIECES // HALVES):
+                v_codes, v_scales = v_mx[q]
+                nc.vector.quantize_mx(
+                    v_codes[:].bitcast(E4M3),
+                    v_scales[:],
+                    v_grouped[:, q * PIECE : (q + 1) * PIECE, :].rearrange("p n j -> p (n j)"),
+                )
+                score_passes(q, v_codes[:], v_scales[:], False)
+                nc.scalar.activation(slopes[q][:], scores[q][:].rearrange("p t n -> p n t"), ACT.Tanh, scale=-1.0)
+                if q == 1:
+                    xm_first = sb.tile([P, P * PACK], BF16, name="xm_first", tag="v1_codes", align_bytes=64)
+                    xm_grouped.append(xm_first[:])
+                    group_xm(0)
 
-        def weigh(h):
-            nc.vector.tensor_tensor(
-                g_grouped[h][:].rearrange("p (c i t) -> p c t i", i=4, t=PACK),
-                slopes[h][:].rearrange("p t (c i) -> p c t i", i=4),
-                weights_wide,
-                MULT,
+        xm_rest = sb.tile([P, D // P - 1, P * PACK], BF16, name="xm_rest", tag="v3_codes", align_bytes=64)
+        xm_grouped.extend(xm_rest[:, u, :] for u in range(D // P - 1))
+
+        weights_wide = row_weights[:].unsqueeze(1).to_broadcast([P, PIECE, PACK])
+
+        def weigh(q):
+            nc.vector.tensor_tensor(g_grouped[q][:], slopes[q][:], weights_wide, MULT)
+
+        def quantize_g(q):
+            slots = slice(HALF + q * PIECE, HALF + (q + 1) * PIECE)
+            nc.vector.quantize_mx(
+                g_codes[:, slots].bitcast(E5M2), g_scales[:, slots], g_grouped[q][:].rearrange("p n t -> p (n t)")
             )
 
-        def quantize_g(h):
-            slots = slice(h * HALF, (h + 1) * HALF)
-            nc.vector.quantize_mx(g_codes[:, slots].bitcast(E5M2), g_scales[:, slots], g_grouped[h][:])
-
-        group_xm(0)
-        group_xm(1)
-        weigh(0)
-        quantize_g(0)
-        weigh(1)
-        quantize_xm(0)
-        quantize_g(1)
-        quantize_xm(1)
-
-        for u in range(D // P):
-            if u >= 2:
-                group_xm(u)
-                quantize_xm(u)
-            grads = psum.tile([P, N], F32, name="grads%d" % u, tag="bank%d" % u)
+        def gradient_pass(name, u, first):
+            grads = psum.tile([P, N], F32, name=name, tag="grads", bufs=4)
             nc.tensor.matmul_mx(
                 grads[:],
                 lhsT=xm_mx[u][0][:].bitcast(E4M3),
                 lhsT_scale=xm_mx[u][1][:],
-                rhs=g_codes[:].bitcast(E5M2),
-                rhs_scale=g_scales[:],
+                rhs=g_codes[:, first : first + N].bitcast(E5M2),
+                rhs_scale=g_scales[:, first : first + N],
                 start=True,
                 stop=True,
             )
+            return grads
+
+        def place_half(grads, h):
+            staged = sb.tile([P, HALF], F32, name="staged_half%d" % h)
+            nc.scalar.copy(staged[:], grads[:, HALF:])
+            nc.vector.tensor_copy(windows[0][:].indirect(half_lists[h]), staged[:])
+
+        weigh(0)
+        weigh(1)
+        quantize_g(0)
+        quantize_xm(0)
+        quantize_g(1)
+        early = gradient_pass("grads_early", 0, 0)
+        weigh(2)
+        weigh(3)
+        group_xm(1)
+        quantize_g(2)
+        quantize_xm(1)
+        quantize_g(3)
+        place_half(early, 0)
+        group_xm(2)
+        place_half(gradient_pass("grads0", 0, HALF), 1)
+        nc.sync.dma_start(out[0:P, :], windows[0][:])
+        group_xm(3)
+        quantize_xm(2)
+        quantize_xm(3)
+
+        for u in range(1, D // P):
+            grads = gradient_pass("grads%d" % u, u, HALF)
             staged = sb.tile([P, N], F32, name="staged%d" % u)
             nc.scalar.copy(staged[:], grads[:])
             nc.vector.tensor_copy(windows[u][:].indirect(offsets[:]), staged[:])

@@ -106,11 +106,11 @@ def tile_attend_gds_lch_kernel(tc, xT, wT, vT, wt, xm, offs, out):
         v_grouped = sb.tile([P, N, PACK], BF16, name="v_grouped", align_bytes=64)
         v_mx = [mx_tiles("v%d" % q, PIECE) for q in range(PIECES)]
         slopes = [sb.tile([P, PIECE, PACK], F32, name="slopes%d" % q) for q in range(PIECES)]
-        g_grouped = [sb.tile([P, PIECE, PACK], BF16, name="g_grouped%d" % q, align_bytes=64) for q in range(PIECES)]
+        g_grouped = [sb.tile([P, PIECE, PACK], BF16, name="g_grouped%d" % q, tag="g_grouped%d" % q, align_bytes=64) for q in range(PIECES)]
         g_codes, g_scales = mx_tiles("g", HALF + N)
         nc.vector.memset(g_codes[:, :HALF], 0)
         nc.vector.memset(g_scales[:, :HALF], 127)
-        xm_mx = [mx_tiles("xm%d" % u, P) for u in range(D // P)]
+        xm_codes, xm_scales = mx_tiles("xm", D)
         xm_grouped = []
 
         def group_xm(u):
@@ -119,32 +119,39 @@ def tile_attend_gds_lch_kernel(tc, xT, wT, vT, wt, xm, offs, out):
                 xm_raw[:, :, u * P : (u + 1) * P].rearrange("p t (c i) -> p c t i", i=4),
             )
 
-        def quantize_xm(u):
-            nc.vector.quantize_mx(xm_mx[u][0][:].bitcast(E4M3), xm_mx[u][1][:], xm_grouped[u])
+        def quantize_xm(u, grouped):
+            cols = slice(u * P, u * P + grouped.shape[1] // PACK)
+            nc.vector.quantize_mx(xm_codes[:, cols].bitcast(E4M3), xm_scales[:, cols], grouped)
 
         for j in range(PACK - 1):
             nc.vector.tensor_copy(v_grouped[:, :, j], v_planes[j][:].indirect(offsets[:]))
-        for h in range(HALVES):
-            first, end = max(0, h * HALF - OVERLAP), (h + 1) * HALF
+
+        def gather_last_plane(first, end):
             nc.vector.tensor_copy(
                 v_grouped[:, first:end, PACK - 1], v_planes[PACK - 1][:].indirect(offsets[:, first // 16 : end // 16])
             )
-            for q in range(h * PIECES // HALVES, (h + 1) * PIECES // HALVES):
-                v_codes, v_scales = v_mx[q]
-                nc.vector.quantize_mx(
-                    v_codes[:].bitcast(E4M3),
-                    v_scales[:],
-                    v_grouped[:, q * PIECE : (q + 1) * PIECE, :].rearrange("p n j -> p (n j)"),
-                )
-                score_passes(q, v_codes[:], v_scales[:], False)
-                nc.scalar.activation(slopes[q][:], scores[q][:].rearrange("p t n -> p n t"), ACT.Tanh, scale=-1.0)
-                if q == 1:
-                    xm_first = sb.tile([P, P * PACK], BF16, name="xm_first", tag="v1_codes", align_bytes=64)
-                    xm_grouped.append(xm_first[:])
-                    group_xm(0)
 
-        xm_rest = sb.tile([P, D // P - 1, P * PACK], BF16, name="xm_rest", tag="v3_codes", align_bytes=64)
-        xm_grouped.extend(xm_rest[:, u, :] for u in range(D // P - 1))
+        def finish_scores(q):
+            v_codes, v_scales = v_mx[q]
+            nc.vector.quantize_mx(
+                v_codes[:].bitcast(E4M3),
+                v_scales[:],
+                v_grouped[:, q * PIECE : (q + 1) * PIECE, :].rearrange("p n j -> p (n j)"),
+            )
+            score_passes(q, v_codes[:], v_scales[:], False)
+            nc.scalar.activation(slopes[q][:], scores[q][:].rearrange("p t n -> p n t"), ACT.Tanh, scale=-1.0)
+
+        gather_last_plane(0, HALF)
+        finish_scores(1)
+        gather_last_plane(HALF - OVERLAP, N)
+        xm_first = sb.tile([P, P * PACK], BF16, name="xm_first", tag="v1_codes", align_bytes=64)
+        xm_grouped.append(xm_first[:])
+        group_xm(0)
+        for q in (0, 2, 3):
+            finish_scores(q)
+
+        xm_second = sb.tile([P, P * PACK], BF16, name="xm_second", tag="v3_codes", align_bytes=64)
+        xm_grouped.append(xm_second[:])
 
         weights_wide = row_weights[:].unsqueeze(1).to_broadcast([P, PIECE, PACK])
 
@@ -161,8 +168,8 @@ def tile_attend_gds_lch_kernel(tc, xT, wT, vT, wt, xm, offs, out):
             grads = psum.tile([P, N], F32, name=name, tag="grads", bufs=4)
             nc.tensor.matmul_mx(
                 grads[:],
-                lhsT=xm_mx[u][0][:].bitcast(E4M3),
-                lhsT_scale=xm_mx[u][1][:],
+                lhsT=xm_codes[:, u * P : (u + 1) * P].bitcast(E4M3),
+                lhsT_scale=xm_scales[:, u * P : (u + 1) * P],
                 rhs=g_codes[:, first : first + N].bitcast(E5M2),
                 rhs_scale=g_scales[:, first : first + N],
                 start=True,
@@ -175,29 +182,34 @@ def tile_attend_gds_lch_kernel(tc, xT, wT, vT, wt, xm, offs, out):
             nc.scalar.copy(staged[:], grads[:, HALF:])
             nc.vector.tensor_copy(windows[0][:].indirect(half_lists[h]), staged[:])
 
-        weigh(0)
         weigh(1)
-        quantize_g(0)
-        quantize_xm(0)
+        quantize_xm(0, xm_grouped[0])
         quantize_g(1)
-        early = gradient_pass("grads_early", 0, 0)
+        weigh(0)
         weigh(2)
+        quantize_g(0)
+        early = gradient_pass("grads_early", 0, 0)
         weigh(3)
         group_xm(1)
         quantize_g(2)
-        quantize_xm(1)
+        quantize_xm(1, xm_grouped[1])
         quantize_g(3)
         place_half(early, 0)
+        xm_rest = sb.tile([P, 2 * P * PACK], BF16, name="xm_rest", tag="g_grouped3", align_bytes=64)
+        xm_grouped.extend([xm_rest[:, : P * PACK], xm_rest[:, P * PACK :]])
         group_xm(2)
         place_half(gradient_pass("grads0", 0, HALF), 1)
         nc.sync.dma_start(out[0:P, :], windows[0][:])
         group_xm(3)
-        quantize_xm(2)
-        quantize_xm(3)
+        quantize_xm(2, xm_rest[:])
 
         for u in range(1, D // P):
             grads = gradient_pass("grads%d" % u, u, HALF)
             staged = sb.tile([P, N], F32, name="staged%d" % u)
             nc.scalar.copy(staged[:], grads[:])
             nc.vector.tensor_copy(windows[u][:].indirect(offsets[:]), staged[:])
-            nc.sync.dma_start(out[u * P : (u + 1) * P, :], windows[u][:])
+            if u < D // P - 1:
+                nc.sync.dma_start(out[u * P : (u + 1) * P, :], windows[u][:])
+            else:
+                nc.sync.dma_start(out[u * P : (u + 1) * P, : T // 2], windows[u][:, : T // 2])
+                nc.scalar.dma_start(out[u * P : (u + 1) * P, T // 2 :], windows[u][:, T // 2 :])

@@ -45,12 +45,13 @@ def tile_attend_gds_lch_kernel(tc, xT, wT, vT, wt, xm, offs, out):
         x_raw = sb.tile([P, PACK, R], F32, name="x_raw")
         nc.sync.dma_start(x_raw[:], xT[0].rearrange("(p j) r -> p j r", j=PACK))
         nc.sync.dma_start(offsets[:], offs)
-        w_planes = [sb.tile([P, T], F32, name="w_plane%d" % j) for j in range(PACK)]
+        w_pairs = [sb.tile([P, 2, T], F32, name="w_pair%d" % e) for e in range(PACK // 2)]
+        w_planes = [w_pairs[j // 2][:, j % 2, :] for j in range(PACK)]
         v_planes = [sb.tile([P, T], F32, name="v_plane%d" % j) for j in range(PACK)]
         w_rows = wT.rearrange("(p j) c -> p j c", j=PACK)
         v_rows = vT.rearrange("(p j) c -> p j c", j=PACK)
-        for j in range(PACK):
-            nc.sync.dma_start(w_planes[j][:], w_rows[:, j, :])
+        for e in range(PACK // 2):
+            nc.sync.dma_start(w_pairs[e][:], w_rows[:, 2 * e : 2 * e + 2, :])
         for j in range(PACK):
             nc.sync.dma_start(v_planes[j][:], v_rows[:, j, :])
         xm_raw = sb.tile([P, PACK, D], F32, name="xm_raw")
@@ -61,7 +62,7 @@ def tile_attend_gds_lch_kernel(tc, xT, wT, vT, wt, xm, offs, out):
 
         windows = [sb.tile([P, T], F32, name="window%d" % u) for u in range(D // P)]
         for window in windows:
-            nc.vector.memset(window[:], 0.0)
+            nc.gpsimd.memset(window[:], 0.0)
 
         x_grouped = sb.tile([P, R * PACK], BF16, name="x_grouped", align_bytes=64)
         nc.scalar.copy(
@@ -73,7 +74,7 @@ def tile_attend_gds_lch_kernel(tc, xT, wT, vT, wt, xm, offs, out):
 
         w_picked = sb.tile([P, PACK, N], F32, name="w_picked")
         for j in range(PACK):
-            nc.vector.tensor_copy(w_picked[:, j, :], w_planes[j][:].indirect(offsets[:]))
+            nc.vector.tensor_copy(w_picked[:, j, :], w_planes[j].indirect(offsets[:]))
         w_grouped = sb.tile([P, N * PACK], BF16, name="w_grouped", align_bytes=64)
         nc.scalar.activation(
             w_grouped[:].rearrange("p (c i j) -> p c j i", i=4, j=PACK),
@@ -108,8 +109,8 @@ def tile_attend_gds_lch_kernel(tc, xT, wT, vT, wt, xm, offs, out):
         slopes = [sb.tile([P, PIECE, PACK], F32, name="slopes%d" % q) for q in range(PIECES)]
         g_grouped = [sb.tile([P, PIECE, PACK], BF16, name="g_grouped%d" % q, tag="g_grouped%d" % q, align_bytes=64) for q in range(PIECES)]
         g_codes, g_scales = mx_tiles("g", HALF + N)
-        nc.vector.memset(g_codes[:, :HALF], 0)
-        nc.vector.memset(g_scales[:, :HALF], 127)
+        nc.gpsimd.memset(g_codes[:, :HALF], 0)
+        nc.gpsimd.memset(g_scales[:, :HALF], 127)
         xm_codes, xm_scales = mx_tiles("xm", D)
         xm_grouped = []
 
@@ -123,8 +124,11 @@ def tile_attend_gds_lch_kernel(tc, xT, wT, vT, wt, xm, offs, out):
             cols = slice(u * P, u * P + grouped.shape[1] // PACK)
             nc.vector.quantize_mx(xm_codes[:, cols].bitcast(E4M3), xm_scales[:, cols], grouped)
 
-        for j in range(PACK - 1):
-            nc.vector.tensor_copy(v_grouped[:, :, j], v_planes[j][:].indirect(offsets[:]))
+        v_picked = sb.tile([P, 2, N], F32, name="v_picked")
+        for j in range(2):
+            nc.vector.tensor_copy(v_picked[:, j, :], v_planes[j][:].indirect(offsets[:]))
+        nc.scalar.copy(v_grouped[:, :, 0:2], v_picked[:].rearrange("p j n -> p n j"))
+        nc.vector.tensor_copy(v_grouped[:, :, 2], v_planes[2][:].indirect(offsets[:]))
 
         def gather_last_plane(first, end):
             nc.vector.tensor_copy(

@@ -14,15 +14,16 @@ E4M3 = mybir.dt.float8_e4m3fn_x4
 E5M2 = mybir.dt.float8_e5m2_x4
 ACT = mybir.ActivationFunctionType
 MULT = mybir.AluOpType.mult
+ADD = mybir.AluOpType.add
 
 P = 128
 PACK = 4
 HALVES = 2
 HALF = N // HALVES
 LIST_COLS = HALF // 16
-OVERLAP = 32
 PIECES = 4
 PIECE = N // PIECES
+PAD = N - PIECE
 
 
 def tile_attend_gds_lch_kernel(tc, xT, wT, vT, wt, xm, offs, out):
@@ -54,8 +55,12 @@ def tile_attend_gds_lch_kernel(tc, xT, wT, vT, wt, xm, offs, out):
             nc.sync.dma_start(w_pairs[e][:], w_rows[:, 2 * e : 2 * e + 2, :])
         for j in range(PACK):
             nc.sync.dma_start(v_planes[j][:], v_rows[:, j, :])
-        xm_raw = sb.tile([P, PACK, D], F32, name="xm_raw")
-        nc.sync.dma_start(xm_raw[:], xm[0].rearrange("(p t) d -> p t d", t=PACK))
+        xm_rows = xm[0].rearrange("(p t) d -> p t d", t=PACK)
+        xm_raw = []
+        for first, end in ((0, 1), (1, 2), (2, 4)):
+            piece = sb.tile([P, PACK, (end - first) * P], F32, name="xm_raw%d" % first)
+            nc.sync.dma_start(piece[:], xm_rows[:, :, first * P : end * P])
+            xm_raw.extend(piece[:, :, u * P : (u + 1) * P] for u in range(end - first))
 
         warm = sb.tile([P, 1], F32, name="warm")
         nc.scalar.activation(warm[:], row_weights[:, 0:1], ACT.Tanh)
@@ -104,114 +109,124 @@ def tile_attend_gds_lch_kernel(tc, xT, wT, vT, wt, xm, offs, out):
             slots = slice(q * PIECE, (q + 1) * PIECE)
             score_passes(q, w_codes[:, slots], w_scales[:, slots], True)
 
-        v_grouped = sb.tile([P, N, PACK], BF16, name="v_grouped", align_bytes=64)
+        v_grouped = sb.tile([P, HALVES, HALVES, PIECE, PACK], BF16, name="v_grouped", align_bytes=64)
+
+        def v_half(h):
+            return v_grouped[:, :, 1 - h, :, :]
+
         v_mx = [mx_tiles("v%d" % q, PIECE) for q in range(PIECES)]
         slopes = [sb.tile([P, PIECE, PACK], F32, name="slopes%d" % q) for q in range(PIECES)]
-        g_grouped = [sb.tile([P, PIECE, PACK], BF16, name="g_grouped%d" % q, tag="g_grouped%d" % q, align_bytes=64) for q in range(PIECES)]
-        g_codes, g_scales = mx_tiles("g", HALF + N)
-        nc.gpsimd.memset(g_codes[:, :HALF], 0)
-        nc.gpsimd.memset(g_scales[:, :HALF], 127)
+        g_grouped = [sb.tile([P, PIECE, PACK], BF16, name="g_grouped%d" % q, align_bytes=64) for q in range(PIECES)]
+        g_codes, g_scales = mx_tiles("g", PAD + N)
+        nc.gpsimd.memset(g_codes[:, :PAD], 0)
+        nc.gpsimd.memset(g_scales[:, :PAD], 127)
+        zeros = sb.tile([P, PIECE], F32, name="zeros")
+        nc.gpsimd.memset(zeros[:], 0.0)
         xm_codes, xm_scales = mx_tiles("xm", D)
         xm_grouped = []
 
         def group_xm(u):
             nc.scalar.copy(
                 xm_grouped[u].rearrange("p (c i t) -> p c t i", i=4, t=PACK),
-                xm_raw[:, :, u * P : (u + 1) * P].rearrange("p t (c i) -> p c t i", i=4),
+                xm_raw[u].rearrange("p t (c i) -> p c t i", i=4),
             )
 
         def quantize_xm(u, grouped):
             cols = slice(u * P, u * P + grouped.shape[1] // PACK)
             nc.vector.quantize_mx(xm_codes[:, cols].bitcast(E4M3), xm_scales[:, cols], grouped)
 
+        def gather_v_plane(j, h):
+            nc.vector.tensor_copy(v_half(h)[:, :, :, j], v_planes[j][:].indirect(half_lists[h]))
+
         v_picked = sb.tile([P, 2, N], F32, name="v_picked")
         for j in range(2):
             nc.vector.tensor_copy(v_picked[:, j, :], v_planes[j][:].indirect(offsets[:]))
-        nc.scalar.copy(v_grouped[:, :, 0:2], v_picked[:].rearrange("p j n -> p n j"))
-        nc.vector.tensor_copy(v_grouped[:, :, 2], v_planes[2][:].indirect(offsets[:]))
-
-        def gather_last_plane(first, end):
-            nc.vector.tensor_copy(
-                v_grouped[:, first:end, PACK - 1], v_planes[PACK - 1][:].indirect(offsets[:, first // 16 : end // 16])
+        for h in range(HALVES):
+            nc.scalar.copy(
+                v_half(h)[:, :, :, 0:2],
+                v_picked[:, :, h * HALF : (h + 1) * HALF].rearrange("p j (k n) -> p k n j", k=HALVES),
             )
+            gather_v_plane(2, h)
 
-        def finish_scores(q):
+        def finish_scores(q, cuts):
             v_codes, v_scales = v_mx[q]
             nc.vector.quantize_mx(
                 v_codes[:].bitcast(E4M3),
                 v_scales[:],
-                v_grouped[:, q * PIECE : (q + 1) * PIECE, :].rearrange("p n j -> p (n j)"),
+                v_half(q // 2)[:, q % 2, :, :].rearrange("p n j -> p (n j)"),
             )
             score_passes(q, v_codes[:], v_scales[:], False)
-            nc.scalar.activation(slopes[q][:], scores[q][:].rearrange("p t n -> p n t"), ACT.Tanh, scale=-1.0)
+            for cut in cuts:
+                nc.scalar.activation(
+                    slopes[q][:, cut, :], scores[q][:, :, cut].rearrange("p t n -> p n t"), ACT.Tanh, scale=-1.0
+                )
 
-        gather_last_plane(0, HALF)
-        finish_scores(1)
-        gather_last_plane(HALF - OVERLAP, N)
-        xm_first = sb.tile([P, P * PACK], BF16, name="xm_first", tag="v1_codes", align_bytes=64)
-        xm_grouped.append(xm_first[:])
-        group_xm(0)
-        for q in (0, 2, 3):
-            finish_scores(q)
+        whole = [slice(0, PIECE)]
+        in_two = [slice(0, PIECE // 2), slice(PIECE // 2, PIECE)]
 
-        xm_second = sb.tile([P, P * PACK], BF16, name="xm_second", tag="v3_codes", align_bytes=64)
-        xm_grouped.append(xm_second[:])
+        gather_v_plane(3, 0)
+        for u in range(2):
+            grouped = sb.tile([P, P * PACK], BF16, name="xm_grouped%d" % u, align_bytes=64)
+            xm_grouped.append(grouped[:])
+            group_xm(u)
+        finish_scores(0, in_two)
+        finish_scores(1, whole)
+        gather_v_plane(3, 1)
+        quantize_xm(0, xm_grouped[0])
+        finish_scores(2, whole)
+        finish_scores(3, whole)
+        quantize_xm(1, xm_grouped[1])
+        xm_rest = sb.tile([P, 2 * P * PACK], BF16, name="xm_rest", tag="v3_codes", align_bytes=64)
+        xm_grouped.extend([xm_rest[:, : P * PACK], xm_rest[:, P * PACK :]])
 
-        weights_wide = row_weights[:].unsqueeze(1).to_broadcast([P, PIECE, PACK])
-
-        def weigh(q):
-            nc.vector.tensor_tensor(g_grouped[q][:], slopes[q][:], weights_wide, MULT)
+        def weigh(q, cuts):
+            for cut in cuts:
+                weights_wide = row_weights[:].unsqueeze(1).to_broadcast([P, cut.stop - cut.start, PACK])
+                nc.vector.tensor_tensor(g_grouped[q][:, cut, :], slopes[q][:, cut, :], weights_wide, MULT)
 
         def quantize_g(q):
-            slots = slice(HALF + q * PIECE, HALF + (q + 1) * PIECE)
+            slots = slice(PAD + q * PIECE, PAD + (q + 1) * PIECE)
             nc.vector.quantize_mx(
                 g_codes[:, slots].bitcast(E5M2), g_scales[:, slots], g_grouped[q][:].rearrange("p n t -> p (n t)")
             )
 
-        def gradient_pass(name, u, first):
-            grads = psum.tile([P, N], F32, name=name, tag="grads", bufs=4)
+        def gradient(u, first, end):
+            grads = psum.tile([P, N], F32, name="grads%d_%d" % (u, end), tag="grads", bufs=4)
+            words = slice(PAD + end - N, PAD + end)
             nc.tensor.matmul_mx(
                 grads[:],
                 lhsT=xm_codes[:, u * P : (u + 1) * P].bitcast(E4M3),
                 lhsT_scale=xm_scales[:, u * P : (u + 1) * P],
-                rhs=g_codes[:, first : first + N].bitcast(E5M2),
-                rhs_scale=g_scales[:, first : first + N],
+                rhs=g_codes[:, words].bitcast(E5M2),
+                rhs_scale=g_scales[:, words],
                 start=True,
                 stop=True,
             )
-            return grads
+            staged = sb.tile([P, end - first], F32, name="staged%d_%d" % (u, end))
+            nc.scalar.copy(staged[:], grads[:, N - (end - first) :])
+            return staged
 
-        def place_half(grads, h):
-            staged = sb.tile([P, HALF], F32, name="staged_half%d" % h)
-            nc.scalar.copy(staged[:], grads[:, HALF:])
-            nc.vector.tensor_copy(windows[0][:].indirect(half_lists[h]), staged[:])
+        def place(u, first, end, staged):
+            nc.vector.tensor_copy(windows[u][:].indirect(offsets[:, first // 16 : end // 16]), staged[:])
 
-        weigh(1)
-        quantize_xm(0, xm_grouped[0])
-        quantize_g(1)
-        weigh(0)
-        weigh(2)
+        weigh(0, in_two)
+        weigh(1, whole)
         quantize_g(0)
-        early = gradient_pass("grads_early", 0, 0)
-        weigh(3)
-        group_xm(1)
-        quantize_g(2)
-        quantize_xm(1, xm_grouped[1])
-        quantize_g(3)
-        place_half(early, 0)
-        xm_rest = sb.tile([P, 2 * P * PACK], BF16, name="xm_rest", tag="g_grouped3", align_bytes=64)
-        xm_grouped.extend([xm_rest[:, : P * PACK], xm_rest[:, P * PACK :]])
+        first_quarter = gradient(0, 0, PIECE)
         group_xm(2)
-        place_half(gradient_pass("grads0", 0, HALF), 1)
-        nc.sync.dma_start(out[0:P, :], windows[0][:])
+        weigh(2, whole)
+        quantize_g(1)
+        first_half = gradient(1, 0, HALF)
         group_xm(3)
+        weigh(3, whole)
+        quantize_g(2)
+        nc.vector.tensor_tensor(windows[0][:].indirect(offsets[:, : PIECE // 16]), first_quarter[:], zeros[:], ADD)
+        quantize_g(3)
         quantize_xm(2, xm_rest[:])
+        place(1, 0, HALF, first_half)
 
-        for u in range(1, D // P):
-            grads = gradient_pass("grads%d" % u, u, HALF)
-            staged = sb.tile([P, N], F32, name="staged%d" % u)
-            nc.scalar.copy(staged[:], grads[:])
-            nc.vector.tensor_copy(windows[u][:].indirect(offsets[:]), staged[:])
+        for u, first in enumerate((PIECE, HALF, 0, 0)):
+            place(u, first, N, gradient(u, first, N))
             if u < D // P - 1:
                 nc.sync.dma_start(out[u * P : (u + 1) * P, :], windows[u][:])
             else:

@@ -20,7 +20,6 @@ P = 128
 PACK = 4
 HALVES = 2
 HALF = N // HALVES
-LIST_COLS = HALF // 16
 PIECES = 4
 PIECE = N // PIECES
 PAD = N - PIECE
@@ -38,7 +37,6 @@ def tile_attend_gds_lch_kernel(tc, xT, wT, vT, wt, xm, offs, out):
             return codes, scales
 
         offsets = sb.tile([P, N // 16], U16, name="offsets")
-        half_lists = [offsets[:, h * LIST_COLS : (h + 1) * LIST_COLS] for h in range(HALVES)]
 
         row_weights = sb.tile([P, PACK], F32, name="row_weights")
         nc.scalar.dma_start(row_weights[:], wt[0].rearrange("(p t) o -> p (t o)", t=PACK))
@@ -135,18 +133,21 @@ def tile_attend_gds_lch_kernel(tc, xT, wT, vT, wt, xm, offs, out):
             cols = slice(u * P, u * P + grouped.shape[1] // PACK)
             nc.vector.quantize_mx(xm_codes[:, cols].bitcast(E4M3), xm_scales[:, cols], grouped)
 
-        def gather_v_plane(j, h):
-            nc.vector.tensor_copy(v_half(h)[:, :, :, j], v_planes[j][:].indirect(half_lists[h]))
-
-        v_picked = sb.tile([P, 2, N], F32, name="v_picked")
+        v_early = sb.tile([P, 2, N], F32, name="v_early")
         for j in range(2):
-            nc.vector.tensor_copy(v_picked[:, j, :], v_planes[j][:].indirect(offsets[:]))
+            nc.vector.tensor_copy(v_early[:, j, :], v_planes[j][:].indirect(offsets[:]))
         for h in range(HALVES):
             nc.scalar.copy(
                 v_half(h)[:, :, :, 0:2],
-                v_picked[:, :, h * HALF : (h + 1) * HALF].rearrange("p j (k n) -> p k n j", k=HALVES),
+                v_early[:, :, h * HALF : (h + 1) * HALF].rearrange("p j (k n) -> p k n j", k=HALVES),
             )
-            gather_v_plane(2, h)
+        v_late = sb.tile([P, 2, N], BF16, name="v_late")
+        nc.vector.tensor_copy(v_late[:, 0, :], v_planes[2][:].indirect(offsets[:]))
+        for q in range(PIECES):
+            nc.vector.tensor_copy(
+                v_late[:, 1, q * PIECE : (q + 1) * PIECE],
+                v_planes[3][:].indirect(offsets[:, q * PIECE // 16 : (q + 1) * PIECE // 16]),
+            )
 
         def finish_scores(q, cuts):
             v_codes, v_scales = v_mx[q]
@@ -164,14 +165,19 @@ def tile_attend_gds_lch_kernel(tc, xT, wT, vT, wt, xm, offs, out):
         whole = [slice(0, PIECE)]
         in_two = [slice(0, PIECE // 2), slice(PIECE // 2, PIECE)]
 
-        gather_v_plane(3, 0)
+        for q in range(2):
+            nc.scalar.copy(
+                v_half(0)[:, q, :, 2:4], v_late[:, :, q * PIECE : (q + 1) * PIECE].rearrange("p j n -> p n j")
+            )
         for u in range(2):
             grouped = sb.tile([P, P * PACK], BF16, name="xm_grouped%d" % u, align_bytes=64)
             xm_grouped.append(grouped[:])
             group_xm(u)
         finish_scores(0, in_two)
         finish_scores(1, whole)
-        gather_v_plane(3, 1)
+        nc.vector.tensor_copy(
+            v_half(1)[:, :, :, 2:4], v_late[:, :, HALF:].rearrange("p j (k n) -> p k n j", k=HALVES)
+        )
         quantize_xm(0, xm_grouped[0])
         finish_scores(2, whole)
         finish_scores(3, whole)

@@ -46,7 +46,7 @@ def tile_attend_gds_lch_kernel(tc, xT, wT, vT, wt, xm, offs, out):
         nc.sync.dma_start(offsets[:], offs)
         w_pairs = [sb.tile([P, 2, T], F32, name="w_pair%d" % e) for e in range(PACK // 2)]
         w_planes = [w_pairs[j // 2][:, j % 2, :] for j in range(PACK)]
-        v_planes = [sb.tile([P, T], F32, name="v_plane%d" % j) for j in range(PACK)]
+        v_planes = [sb.tile([P, T], F32, name="v_plane%d" % j, tag="v_plane%d" % j, align_bytes=64) for j in range(PACK)]
         w_rows = wT.rearrange("(p j) c -> p j c", j=PACK)
         v_rows = vT.rearrange("(p j) c -> p j c", j=PACK)
         for e in range(PACK // 2):
@@ -55,13 +55,10 @@ def tile_attend_gds_lch_kernel(tc, xT, wT, vT, wt, xm, offs, out):
             nc.sync.dma_start(v_planes[j][:], v_rows[:, j, :])
         xm_rows = xm[0].rearrange("(p t) d -> p t d", t=PACK)
         xm_raw = []
-        for first, end in ((0, 1), (1, 2), (2, 4)):
+        for first, end in ((0, 1), (1, 4)):
             piece = sb.tile([P, PACK, (end - first) * P], F32, name="xm_raw%d" % first)
             nc.sync.dma_start(piece[:], xm_rows[:, :, first * P : end * P])
             xm_raw.extend(piece[:, :, u * P : (u + 1) * P] for u in range(end - first))
-
-        warm = sb.tile([P, 1], F32, name="warm")
-        nc.scalar.activation(warm[:], row_weights[:, 0:1], ACT.Tanh)
 
         windows = [sb.tile([P, T], F32, name="window%d" % u) for u in range(D // P)]
         for window in windows:
@@ -85,9 +82,6 @@ def tile_attend_gds_lch_kernel(tc, xT, wT, vT, wt, xm, offs, out):
             ACT.Copy,
             scale=-1.0,
         )
-        w_codes, w_scales = mx_tiles("w", N)
-        nc.vector.quantize_mx(w_codes[:].bitcast(E4M3), w_scales[:], w_grouped[:])
-
         scores = [psum.tile([P, PACK, PIECE], F32, name="scores%d" % q) for q in range(PIECES)]
 
         def score_passes(q, codes, scales, opens):
@@ -103,9 +97,9 @@ def tile_attend_gds_lch_kernel(tc, xT, wT, vT, wt, xm, offs, out):
                     stop=(not opens and t == PACK - 1),
                 )
 
-        for q in range(PIECES):
-            slots = slice(q * PIECE, (q + 1) * PIECE)
-            score_passes(q, w_codes[:, slots], w_scales[:, slots], True)
+        w_last_codes, w_last_scales = mx_tiles("w_last", PIECE)
+        nc.vector.quantize_mx(w_last_codes[:].bitcast(E4M3), w_last_scales[:], w_grouped[:, PAD * PACK :])
+        score_passes(PIECES - 1, w_last_codes[:], w_last_scales[:], True)
 
         v_grouped = sb.tile([P, HALVES, HALVES, PIECE, PACK], BF16, name="v_grouped", align_bytes=64)
 
@@ -143,11 +137,17 @@ def tile_attend_gds_lch_kernel(tc, xT, wT, vT, wt, xm, offs, out):
             )
         v_late = sb.tile([P, 2, N], BF16, name="v_late")
         nc.vector.tensor_copy(v_late[:, 0, :], v_planes[2][:].indirect(offsets[:]))
-        for q in range(PIECES):
-            nc.vector.tensor_copy(
-                v_late[:, 1, q * PIECE : (q + 1) * PIECE],
-                v_planes[3][:].indirect(offsets[:, q * PIECE // 16 : (q + 1) * PIECE // 16]),
+        w_codes = sb.tile([P, PAD], U32, name="w_codes", tag="v_plane2", align_bytes=64)
+        w_scales = sb.tile([P, PAD], U8, name="w_scales", align_bytes=64)
+        for first, end in ((0, HALF), (HALF, PAD)):
+            nc.vector.quantize_mx(
+                w_codes[:, first:end].bitcast(E4M3), w_scales[:, first:end], w_grouped[:, first * PACK : end * PACK]
             )
+        for q in range(PIECES - 1):
+            slots = slice(q * PIECE, (q + 1) * PIECE)
+            score_passes(q, w_codes[:, slots], w_scales[:, slots], True)
+        for first, end in ((0, PIECE), (PIECE, HALF), (HALF, N)):
+            nc.vector.tensor_copy(v_late[:, 1, first:end], v_planes[3][:].indirect(offsets[:, first // 16 : end // 16]))
 
         def finish_scores(q, cuts):
             v_codes, v_scales = v_mx[q]
@@ -169,10 +169,9 @@ def tile_attend_gds_lch_kernel(tc, xT, wT, vT, wt, xm, offs, out):
             nc.scalar.copy(
                 v_half(0)[:, q, :, 2:4], v_late[:, :, q * PIECE : (q + 1) * PIECE].rearrange("p j n -> p n j")
             )
-        for u in range(2):
-            grouped = sb.tile([P, P * PACK], BF16, name="xm_grouped%d" % u, align_bytes=64)
-            xm_grouped.append(grouped[:])
-            group_xm(u)
+        xm_first = sb.tile([P, P * PACK], BF16, name="xm_first", align_bytes=64)
+        xm_grouped.append(xm_first[:])
+        group_xm(0)
         finish_scores(0, in_two)
         finish_scores(1, whole)
         nc.vector.tensor_copy(
@@ -181,9 +180,8 @@ def tile_attend_gds_lch_kernel(tc, xT, wT, vT, wt, xm, offs, out):
         quantize_xm(0, xm_grouped[0])
         finish_scores(2, whole)
         finish_scores(3, whole)
-        quantize_xm(1, xm_grouped[1])
-        xm_rest = sb.tile([P, 2 * P * PACK], BF16, name="xm_rest", tag="v3_codes", align_bytes=64)
-        xm_grouped.extend([xm_rest[:, : P * PACK], xm_rest[:, P * PACK :]])
+        xm_rest = sb.tile([P, (PACK - 1) * P * PACK], BF16, name="xm_rest", tag="v3_codes", align_bytes=64)
+        xm_grouped.extend(xm_rest[:, k * P * PACK : (k + 1) * P * PACK] for k in range(PACK - 1))
 
         def weigh(q, cuts):
             for cut in cuts:
@@ -215,23 +213,30 @@ def tile_attend_gds_lch_kernel(tc, xT, wT, vT, wt, xm, offs, out):
         def place(u, first, end, staged):
             nc.vector.tensor_copy(windows[u][:].indirect(offsets[:, first // 16 : end // 16]), staged[:])
 
+        def place_quarter(q, staged):
+            nc.vector.tensor_tensor(
+                windows[0][:].indirect(offsets[:, q * PIECE // 16 : (q + 1) * PIECE // 16]), staged[:], zeros[:], ADD
+            )
+
         weigh(0, in_two)
         weigh(1, whole)
         quantize_g(0)
         first_quarter = gradient(0, 0, PIECE)
-        group_xm(2)
         weigh(2, whole)
         quantize_g(1)
-        first_half = gradient(1, 0, HALF)
-        group_xm(3)
+        second_quarter = gradient(0, PIECE, HALF)
         weigh(3, whole)
         quantize_g(2)
-        nc.vector.tensor_tensor(windows[0][:].indirect(offsets[:, : PIECE // 16]), first_quarter[:], zeros[:], ADD)
+        place_quarter(0, first_quarter)
         quantize_g(3)
-        quantize_xm(2, xm_rest[:])
-        place(1, 0, HALF, first_half)
+        place_quarter(1, second_quarter)
+        group_xm(1)
+        quantize_xm(1, xm_grouped[1])
+        group_xm(2)
+        group_xm(3)
+        quantize_xm(2, xm_rest[:, P * PACK :])
 
-        for u, first in enumerate((PIECE, HALF, 0, 0)):
+        for u, first in enumerate((HALF, 0, 0, 0)):
             place(u, first, N, gradient(u, first, N))
             if u < D // P - 1:
                 nc.sync.dma_start(out[u * P : (u + 1) * P, :], windows[u][:])

@@ -46,7 +46,7 @@ def tile_attend_gds_lch_kernel(tc, xT, wT, vT, wt, xm, offs, out):
         nc.sync.dma_start(offsets[:], offs)
         w_pairs = [sb.tile([P, 2, T], F32, name="w_pair%d" % e) for e in range(PACK // 2)]
         w_planes = [w_pairs[j // 2][:, j % 2, :] for j in range(PACK)]
-        v_planes = [sb.tile([P, T], F32, name="v_plane%d" % j, tag="v_plane%d" % j, align_bytes=64) for j in range(PACK)]
+        v_planes = [sb.tile([P, T], F32, name="v_plane%d" % j) for j in range(PACK)]
         w_rows = wT.rearrange("(p j) c -> p j c", j=PACK)
         v_rows = vT.rearrange("(p j) c -> p j c", j=PACK)
         for e in range(PACK // 2):
@@ -97,9 +97,11 @@ def tile_attend_gds_lch_kernel(tc, xT, wT, vT, wt, xm, offs, out):
                     stop=(not opens and t == PACK - 1),
                 )
 
-        w_last_codes, w_last_scales = mx_tiles("w_last", PIECE)
-        nc.vector.quantize_mx(w_last_codes[:].bitcast(E4M3), w_last_scales[:], w_grouped[:, PAD * PACK :])
-        score_passes(PIECES - 1, w_last_codes[:], w_last_scales[:], True)
+        w_codes, w_scales = mx_tiles("w", N)
+        nc.vector.quantize_mx(w_codes[:].bitcast(E4M3), w_scales[:], w_grouped[:])
+        for q in range(PIECES):
+            slots = slice(q * PIECE, (q + 1) * PIECE)
+            score_passes(q, w_codes[:, slots], w_scales[:, slots], True)
 
         v_grouped = sb.tile([P, HALVES, HALVES, PIECE, PACK], BF16, name="v_grouped", align_bytes=64)
 
@@ -137,15 +139,6 @@ def tile_attend_gds_lch_kernel(tc, xT, wT, vT, wt, xm, offs, out):
             )
         v_late = sb.tile([P, 2, N], BF16, name="v_late")
         nc.vector.tensor_copy(v_late[:, 0, :], v_planes[2][:].indirect(offsets[:]))
-        w_codes = sb.tile([P, PAD], U32, name="w_codes", tag="v_plane2", align_bytes=64)
-        w_scales = sb.tile([P, PAD], U8, name="w_scales", align_bytes=64)
-        for first, end in ((0, HALF), (HALF, PAD)):
-            nc.vector.quantize_mx(
-                w_codes[:, first:end].bitcast(E4M3), w_scales[:, first:end], w_grouped[:, first * PACK : end * PACK]
-            )
-        for q in range(PIECES - 1):
-            slots = slice(q * PIECE, (q + 1) * PIECE)
-            score_passes(q, w_codes[:, slots], w_scales[:, slots], True)
         for first, end in ((0, PIECE), (PIECE, HALF), (HALF, N)):
             nc.vector.tensor_copy(v_late[:, 1, first:end], v_planes[3][:].indirect(offsets[:, first // 16 : end // 16]))
 

@@ -97,12 +97,6 @@ def tile_attend_gds_lch_kernel(tc, xT, wT, vT, wt, xm, offs, out):
                     stop=(not opens and t == PACK - 1),
                 )
 
-        w_codes, w_scales = mx_tiles("w", N)
-        nc.vector.quantize_mx(w_codes[:].bitcast(E4M3), w_scales[:], w_grouped[:])
-        for q in range(PIECES):
-            slots = slice(q * PIECE, (q + 1) * PIECE)
-            score_passes(q, w_codes[:, slots], w_scales[:, slots], True)
-
         v_grouped = sb.tile([P, HALVES, HALVES, PIECE, PACK], BF16, name="v_grouped", align_bytes=64)
 
         def v_half(h):
@@ -129,14 +123,22 @@ def tile_attend_gds_lch_kernel(tc, xT, wT, vT, wt, xm, offs, out):
             cols = slice(u * P, u * P + grouped.shape[1] // PACK)
             nc.vector.quantize_mx(xm_codes[:, cols].bitcast(E4M3), xm_scales[:, cols], grouped)
 
-        v_early = sb.tile([P, 2, N], F32, name="v_early")
+        v_early = [
+            sb.tile([P, 2, HALF], F32, name="v_early%d" % h, tag="v_early%d" % h, align_bytes=64) for h in range(HALVES)
+        ]
         for j in range(2):
-            nc.vector.tensor_copy(v_early[:, j, :], v_planes[j][:].indirect(offsets[:]))
+            for h in range(HALVES):
+                nc.vector.tensor_copy(
+                    v_early[h][:, j, :], v_planes[j][:].indirect(offsets[:, h * HALF // 16 : (h + 1) * HALF // 16])
+                )
         for h in range(HALVES):
-            nc.scalar.copy(
-                v_half(h)[:, :, :, 0:2],
-                v_early[:, :, h * HALF : (h + 1) * HALF].rearrange("p j (k n) -> p k n j", k=HALVES),
-            )
+            nc.scalar.copy(v_half(h)[:, :, :, 0:2], v_early[h][:].rearrange("p j (k n) -> p k n j", k=HALVES))
+        w_codes = sb.tile([P, N], U32, name="w_codes", tag="v_early0", align_bytes=64)
+        w_scales = sb.tile([P, N], U8, name="w_scales", align_bytes=64)
+        nc.vector.quantize_mx(w_codes[:].bitcast(E4M3), w_scales[:], w_grouped[:])
+        for q in range(PIECES):
+            slots = slice(q * PIECE, (q + 1) * PIECE)
+            score_passes(q, w_codes[:, slots], w_scales[:, slots], True)
         v_late = sb.tile([P, 2, N], BF16, name="v_late")
         nc.vector.tensor_copy(v_late[:, 0, :], v_planes[2][:].indirect(offsets[:]))
         for first, end in ((0, PIECE), (PIECE, HALF), (HALF, N)):

@@ -55,7 +55,7 @@ def tile_attend_gds_lch_kernel(tc, xT, wT, vT, wt, xm, offs, out):
             nc.sync.dma_start(v_planes[j][:], v_rows[:, j, :])
         xm_rows = xm[0].rearrange("(p t) d -> p t d", t=PACK)
         xm_raw = []
-        for first, end in ((0, 1), (1, 4)):
+        for first, end in ((0, 1), (1, 2), (2, 4)):
             piece = sb.tile([P, PACK, (end - first) * P], F32, name="xm_raw%d" % first)
             nc.sync.dma_start(piece[:], xm_rows[:, :, first * P : end * P])
             xm_raw.extend(piece[:, :, u * P : (u + 1) * P] for u in range(end - first))
@@ -164,9 +164,10 @@ def tile_attend_gds_lch_kernel(tc, xT, wT, vT, wt, xm, offs, out):
             nc.scalar.copy(
                 v_half(0)[:, q, :, 2:4], v_late[:, :, q * PIECE : (q + 1) * PIECE].rearrange("p j n -> p n j")
             )
-        xm_first = sb.tile([P, P * PACK], BF16, name="xm_first", align_bytes=64)
-        xm_grouped.append(xm_first[:])
-        group_xm(0)
+        for u in range(2):
+            grouped = sb.tile([P, P * PACK], BF16, name="xm_grouped%d" % u, align_bytes=64)
+            xm_grouped.append(grouped[:])
+            group_xm(u)
         finish_scores(0, in_two)
         finish_scores(1, whole)
         nc.vector.tensor_copy(
@@ -175,8 +176,9 @@ def tile_attend_gds_lch_kernel(tc, xT, wT, vT, wt, xm, offs, out):
         quantize_xm(0, xm_grouped[0])
         finish_scores(2, whole)
         finish_scores(3, whole)
-        xm_rest = sb.tile([P, (PACK - 1) * P * PACK], BF16, name="xm_rest", tag="v3_codes", align_bytes=64)
-        xm_grouped.extend(xm_rest[:, k * P * PACK : (k + 1) * P * PACK] for k in range(PACK - 1))
+        quantize_xm(1, xm_grouped[1])
+        xm_rest = sb.tile([P, 2 * P * PACK], BF16, name="xm_rest", tag="v3_codes", align_bytes=64)
+        xm_grouped.extend([xm_rest[:, : P * PACK], xm_rest[:, P * PACK :]])
 
         def weigh(q, cuts):
             for cut in cuts:
@@ -208,30 +210,23 @@ def tile_attend_gds_lch_kernel(tc, xT, wT, vT, wt, xm, offs, out):
         def place(u, first, end, staged):
             nc.vector.tensor_copy(windows[u][:].indirect(offsets[:, first // 16 : end // 16]), staged[:])
 
-        def place_quarter(q, staged):
-            nc.vector.tensor_tensor(
-                windows[0][:].indirect(offsets[:, q * PIECE // 16 : (q + 1) * PIECE // 16]), staged[:], zeros[:], ADD
-            )
-
         weigh(0, in_two)
         weigh(1, whole)
         quantize_g(0)
         first_quarter = gradient(0, 0, PIECE)
+        group_xm(2)
         weigh(2, whole)
         quantize_g(1)
-        second_quarter = gradient(0, PIECE, HALF)
+        first_half = gradient(1, 0, HALF)
+        group_xm(3)
         weigh(3, whole)
         quantize_g(2)
-        place_quarter(0, first_quarter)
+        nc.vector.tensor_tensor(windows[0][:].indirect(offsets[:, : PIECE // 16]), first_quarter[:], zeros[:], ADD)
         quantize_g(3)
-        place_quarter(1, second_quarter)
-        group_xm(1)
-        quantize_xm(1, xm_grouped[1])
-        group_xm(2)
-        group_xm(3)
-        quantize_xm(2, xm_rest[:, P * PACK :])
+        quantize_xm(2, xm_rest[:])
+        place(1, 0, HALF, first_half)
 
-        for u, first in enumerate((HALF, 0, 0, 0)):
+        for u, first in enumerate((PIECE, HALF, 0, 0)):
             place(u, first, N, gradient(u, first, N))
             if u < D // P - 1:
                 nc.sync.dma_start(out[u * P : (u + 1) * P, :], windows[u][:])

@@ -228,8 +228,4 @@ def tile_attend_gds_lch_kernel(tc, xT, wT, vT, wt, xm, offs, out):
 
         for u, first in enumerate((PIECE, HALF, 0, 0)):
             place(u, first, N, gradient(u, first, N))
-            if u < D // P - 1:
-                nc.sync.dma_start(out[u * P : (u + 1) * P, :], windows[u][:])
-            else:
-                nc.sync.dma_start(out[u * P : (u + 1) * P, : T // 2], windows[u][:, : T // 2])
-                nc.scalar.dma_start(out[u * P : (u + 1) * P, T // 2 :], windows[u][:, T // 2 :])
+            nc.sync.dma_start(out[u * P : (u + 1) * P, :], windows[u][:])

@@ -39,18 +39,15 @@ def tile_attend_gds_lch_kernel(tc, xT, wT, vT, wt, xm, offs, out):
         offsets = sb.tile([P, N // 16], U16, name="offsets")
 
         row_weights = sb.tile([P, PACK], F32, name="row_weights")
-        nc.scalar.dma_start(row_weights[:], wt[0].rearrange("(p t) o -> p (t o)", t=PACK))
 
-        x_raw = sb.tile([P, PACK, R], F32, name="x_raw")
-        nc.sync.dma_start(x_raw[:], xT[0].rearrange("(p j) r -> p j r", j=PACK))
+        w_raw = sb.tile([P, PACK, T], F32, name="w_raw")
+        nc.sync.dma_start(w_raw[:], wT.rearrange("(p j) c -> p j c", j=PACK))
         nc.sync.dma_start(offsets[:], offs)
-        w_pairs = [sb.tile([P, 2, T], F32, name="w_pair%d" % e) for e in range(PACK // 2)]
-        w_planes = [w_pairs[j // 2][:, j % 2, :] for j in range(PACK)]
+        x_raw = sb.tile([P, PACK, R], F32, name="x_raw", tag="x_raw", align_bytes=64)
+        nc.sync.dma_start(x_raw[:], xT[0].rearrange("(p j) r -> p j r", j=PACK))
+        w_planes = [w_raw[:, j, :] for j in range(PACK)]
         v_planes = [sb.tile([P, T], F32, name="v_plane%d" % j) for j in range(PACK)]
-        w_rows = wT.rearrange("(p j) c -> p j c", j=PACK)
         v_rows = vT.rearrange("(p j) c -> p j c", j=PACK)
-        for e in range(PACK // 2):
-            nc.sync.dma_start(w_pairs[e][:], w_rows[:, 2 * e : 2 * e + 2, :])
         for j in range(PACK):
             nc.sync.dma_start(v_planes[j][:], v_rows[:, j, :])
         xm_rows = xm[0].rearrange("(p t) d -> p t d", t=PACK)
@@ -59,6 +56,8 @@ def tile_attend_gds_lch_kernel(tc, xT, wT, vT, wt, xm, offs, out):
             piece = sb.tile([P, PACK, (end - first) * P], F32, name="xm_raw%d" % first)
             nc.sync.dma_start(piece[:], xm_rows[:, :, first * P : end * P])
             xm_raw.extend(piece[:, :, u * P : (u + 1) * P] for u in range(end - first))
+            if first == 0:
+                nc.sync.dma_start(row_weights[:], wt[0].rearrange("(p t) o -> p (t o)", t=PACK))
 
         windows = [sb.tile([P, T], F32, name="window%d" % u) for u in range(D // P)]
         for window in windows:
@@ -75,7 +74,7 @@ def tile_attend_gds_lch_kernel(tc, xT, wT, vT, wt, xm, offs, out):
         w_picked = sb.tile([P, PACK, N], F32, name="w_picked")
         for j in range(PACK):
             nc.vector.tensor_copy(w_picked[:, j, :], w_planes[j].indirect(offsets[:]))
-        w_grouped = sb.tile([P, N * PACK], BF16, name="w_grouped", align_bytes=64)
+        w_grouped = sb.tile([P, N * PACK], BF16, name="w_grouped", tag="x_raw", align_bytes=64)
         nc.scalar.activation(
             w_grouped[:].rearrange("p (c i j) -> p c j i", i=4, j=PACK),
             w_picked[:].rearrange("p j (c i) -> p c j i", i=4),

@@ -103,7 +103,10 @@ def tile_attend_gds_lch_kernel(tc, xT, wT, vT, wt, xm, offs, out):
 
         v_mx = [mx_tiles("v%d" % q, PIECE) for q in range(PIECES)]
         slopes = [sb.tile([P, PIECE, PACK], F32, name="slopes%d" % q) for q in range(PIECES)]
-        g_grouped = [sb.tile([P, PIECE, PACK], BF16, name="g_grouped%d" % q, align_bytes=64) for q in range(PIECES)]
+        g_grouped = [
+            sb.tile([P, PIECE, PACK], BF16, name="g_grouped%d" % q, tag="g_grouped%d" % q, align_bytes=64)
+            for q in range(PIECES)
+        ]
         g_codes, g_scales = mx_tiles("g", PAD + N)
         nc.gpsimd.memset(g_codes[:, :PAD], 0)
         nc.gpsimd.memset(g_scales[:, :PAD], 127)
@@ -163,21 +166,20 @@ def tile_attend_gds_lch_kernel(tc, xT, wT, vT, wt, xm, offs, out):
             nc.scalar.copy(
                 v_half(0)[:, q, :, 2:4], v_late[:, :, q * PIECE : (q + 1) * PIECE].rearrange("p j n -> p n j")
             )
-        for u in range(2):
-            grouped = sb.tile([P, P * PACK], BF16, name="xm_grouped%d" % u, align_bytes=64)
-            xm_grouped.append(grouped[:])
-            group_xm(u)
+        xm_first = sb.tile([P, P * PACK], BF16, name="xm_first", align_bytes=64)
+        xm_grouped.append(xm_first[:])
+        group_xm(0)
         finish_scores(0, in_two)
         finish_scores(1, whole)
+        xm_second = sb.tile([P, P * PACK], BF16, name="xm_second", tag="v1_codes", align_bytes=64)
+        xm_grouped.append(xm_second[:])
+        group_xm(1)
         nc.vector.tensor_copy(
             v_half(1)[:, :, :, 2:4], v_late[:, :, HALF:].rearrange("p j (k n) -> p k n j", k=HALVES)
         )
         quantize_xm(0, xm_grouped[0])
         finish_scores(2, whole)
         finish_scores(3, whole)
-        quantize_xm(1, xm_grouped[1])
-        xm_rest = sb.tile([P, 2 * P * PACK], BF16, name="xm_rest", tag="v3_codes", align_bytes=64)
-        xm_grouped.extend([xm_rest[:, : P * PACK], xm_rest[:, P * PACK :]])
 
         def weigh(q, cuts):
             for cut in cuts:
@@ -213,17 +215,20 @@ def tile_attend_gds_lch_kernel(tc, xT, wT, vT, wt, xm, offs, out):
         weigh(1, whole)
         quantize_g(0)
         first_quarter = gradient(0, 0, PIECE)
-        group_xm(2)
-        weigh(2, whole)
+        quantize_xm(1, xm_grouped[1])
         quantize_g(1)
         first_half = gradient(1, 0, HALF)
-        group_xm(3)
+        weigh(2, whole)
         weigh(3, whole)
         quantize_g(2)
+        xm_rest = sb.tile([P, 2 * P * PACK], BF16, name="xm_rest", tag="g_grouped2", align_bytes=64)
+        xm_grouped.extend([xm_rest[:, : P * PACK], xm_rest[:, P * PACK :]])
+        group_xm(2)
+        group_xm(3)
         nc.vector.tensor_tensor(windows[0][:].indirect(offsets[:, : PIECE // 16]), first_quarter[:], zeros[:], ADD)
         quantize_g(3)
-        quantize_xm(2, xm_rest[:])
         place(1, 0, HALF, first_half)
+        quantize_xm(2, xm_rest[:])
 
         for u, first in enumerate((PIECE, HALF, 0, 0)):
             place(u, first, N, gradient(u, first, N))

@@ -102,7 +102,7 @@ def tile_attend_gds_lch_kernel(tc, xT, wT, vT, wt, xm, offs, out):
             return v_grouped[:, :, 1 - h, :, :]
 
         v_mx = [mx_tiles("v%d" % q, PIECE) for q in range(PIECES)]
-        slopes = [sb.tile([P, PIECE, PACK], F32, name="slopes%d" % q) for q in range(PIECES)]
+        slopes = [sb.tile([P, PIECE, PACK], F32, name="slopes%d" % q) for q in range(PIECES - 1)]
         g_grouped = [
             sb.tile([P, PIECE, PACK], BF16, name="g_grouped%d" % q, tag="g_grouped%d" % q, align_bytes=64)
             for q in range(PIECES)
@@ -154,6 +154,9 @@ def tile_attend_gds_lch_kernel(tc, xT, wT, vT, wt, xm, offs, out):
                 v_half(q // 2)[:, q % 2, :, :].rearrange("p n j -> p (n j)"),
             )
             score_passes(q, v_codes[:], v_scales[:], False)
+            slopes_of(q, cuts)
+
+        def slopes_of(q, cuts):
             for cut in cuts:
                 nc.scalar.activation(
                     slopes[q][:, cut, :], scores[q][:, :, cut].rearrange("p t n -> p n t"), ACT.Tanh, scale=-1.0
@@ -170,7 +173,7 @@ def tile_attend_gds_lch_kernel(tc, xT, wT, vT, wt, xm, offs, out):
         xm_grouped.append(xm_first[:])
         group_xm(0)
         finish_scores(0, in_two)
-        finish_scores(1, whole)
+        finish_scores(1, in_two)
         xm_second = sb.tile([P, P * PACK], BF16, name="xm_second", tag="v1_codes", align_bytes=64)
         xm_grouped.append(xm_second[:])
         group_xm(1)
@@ -179,7 +182,7 @@ def tile_attend_gds_lch_kernel(tc, xT, wT, vT, wt, xm, offs, out):
         )
         quantize_xm(0, xm_grouped[0])
         finish_scores(2, whole)
-        finish_scores(3, whole)
+        finish_scores(3, [])
 
         def weigh(q, cuts):
             for cut in cuts:
@@ -192,7 +195,7 @@ def tile_attend_gds_lch_kernel(tc, xT, wT, vT, wt, xm, offs, out):
                 g_codes[:, slots].bitcast(E5M2), g_scales[:, slots], g_grouped[q][:].rearrange("p n t -> p (n t)")
             )
 
-        def gradient(u, first, end):
+        def gradient(u, first, end, tag=None):
             grads = psum.tile([P, N], F32, name="grads%d_%d" % (u, end), tag="grads", bufs=4)
             words = slice(PAD + end - N, PAD + end)
             nc.tensor.matmul_mx(
@@ -204,32 +207,50 @@ def tile_attend_gds_lch_kernel(tc, xT, wT, vT, wt, xm, offs, out):
                 start=True,
                 stop=True,
             )
-            staged = sb.tile([P, end - first], F32, name="staged%d_%d" % (u, end))
+            name = "staged%d_%d" % (u, end)
+            staged = sb.tile([P, end - first], F32, name=name, tag=tag or name)
             nc.scalar.copy(staged[:], grads[:, N - (end - first) :])
             return staged
 
         def place(u, first, end, staged):
-            nc.vector.tensor_copy(windows[u][:].indirect(offsets[:, first // 16 : end // 16]), staged[:])
+            window = windows[u][:].indirect(offsets[:, first // 16 : end // 16])
+            if end - first == PIECE:
+                nc.vector.tensor_tensor(window, staged[:], zeros[:], ADD)
+            else:
+                nc.vector.tensor_copy(window, staged[:])
 
         weigh(0, in_two)
-        weigh(1, whole)
+        weigh(1, in_two[:1])
         quantize_g(0)
+        weigh(1, in_two[1:])
         first_quarter = gradient(0, 0, PIECE)
+        last_slopes = sb.tile([P, PACK, PIECE], F32, name="last_slopes", tag="last_slopes", align_bytes=64)
+        nc.scalar.activation(last_slopes[:], scores[3][:], ACT.Tanh, scale=-1.0)
         quantize_xm(1, xm_grouped[1])
         quantize_g(1)
         first_half = gradient(1, 0, HALF)
         weigh(2, whole)
-        weigh(3, whole)
+        place(0, 0, PIECE, first_quarter)
         quantize_g(2)
-        xm_rest = sb.tile([P, 2 * P * PACK], BF16, name="xm_rest", tag="g_grouped2", align_bytes=64)
+        place(1, 0, HALF, first_half)
+        pairs = sb.tile([P, 2, PIECE, 2], BF16, name="pairs", tag="pairs")
+        for t in range(PACK):
+            nc.scalar.activation(
+                pairs[:, t // 2, :, t % 2], last_slopes[:, t, :], ACT.Copy, scale=row_weights[:, t : t + 1]
+            )
+        nc.scalar.copy(
+            g_grouped[3][:].rearrange("p n t -> p (n t)").bitcast(U32).rearrange("p (n u) -> p n u", u=2),
+            pairs[:].rearrange("p u n e -> p (u n e)").bitcast(U32).rearrange("p (u n) -> p n u", u=2),
+        )
+        quantize_g(3)
+        middle = gradient(0, PIECE, 3 * PIECE, "pairs")
+        xm_rest = sb.tile([P, 2 * P * PACK], BF16, name="xm_rest", tag="last_slopes", align_bytes=64)
         xm_grouped.extend([xm_rest[:, : P * PACK], xm_rest[:, P * PACK :]])
         group_xm(2)
         group_xm(3)
-        nc.vector.tensor_tensor(windows[0][:].indirect(offsets[:, : PIECE // 16]), first_quarter[:], zeros[:], ADD)
-        quantize_g(3)
-        place(1, 0, HALF, first_half)
+        place(0, PIECE, 3 * PIECE, middle)
         quantize_xm(2, xm_rest[:])
 
-        for u, first in enumerate((PIECE, HALF, 0, 0)):
+        for u, first in ((1, HALF), (0, 3 * PIECE), (2, 0), (3, 0)):
             place(u, first, N, gradient(u, first, N))
             nc.sync.dma_start(out[u * P : (u + 1) * P, :], windows[u][:])

@@ -195,7 +195,7 @@ def tile_attend_gds_lch_kernel(tc, xT, wT, vT, wt, xm, offs, out):
                 g_codes[:, slots].bitcast(E5M2), g_scales[:, slots], g_grouped[q][:].rearrange("p n t -> p (n t)")
             )
 
-        def gradient(u, first, end, tag=None):
+        def gradient(u, first, end, staged=None):
             grads = psum.tile([P, N], F32, name="grads%d_%d" % (u, end), tag="grads", bufs=4)
             words = slice(PAD + end - N, PAD + end)
             nc.tensor.matmul_mx(
@@ -207,17 +207,17 @@ def tile_attend_gds_lch_kernel(tc, xT, wT, vT, wt, xm, offs, out):
                 start=True,
                 stop=True,
             )
-            name = "staged%d_%d" % (u, end)
-            staged = sb.tile([P, end - first], F32, name=name, tag=tag or name)
-            nc.scalar.copy(staged[:], grads[:, N - (end - first) :])
+            if staged is None:
+                staged = sb.tile([P, end - first], F32, name="staged%d_%d" % (u, end))[:]
+            nc.scalar.copy(staged, grads[:, N - (end - first) :])
             return staged
 
         def place(u, first, end, staged):
             window = windows[u][:].indirect(offsets[:, first // 16 : end // 16])
             if end - first == PIECE:
-                nc.vector.tensor_tensor(window, staged[:], zeros[:], ADD)
+                nc.vector.tensor_tensor(window, staged, zeros[:], ADD)
             else:
-                nc.vector.tensor_copy(window, staged[:])
+                nc.vector.tensor_copy(window, staged)
 
         weigh(0, in_two)
         weigh(1, in_two[:1])
@@ -233,7 +233,7 @@ def tile_attend_gds_lch_kernel(tc, xT, wT, vT, wt, xm, offs, out):
         place(0, 0, PIECE, first_quarter)
         quantize_g(2)
         place(1, 0, HALF, first_half)
-        pairs = sb.tile([P, 2, PIECE, 2], BF16, name="pairs", tag="pairs")
+        pairs = sb.tile([P, 2, PIECE, 2], BF16, name="pairs", tag="pairs", align_bytes=64)
         for t in range(PACK):
             nc.scalar.activation(
                 pairs[:, t // 2, :, t % 2], last_slopes[:, t, :], ACT.Copy, scale=row_weights[:, t : t + 1]
@@ -243,14 +243,15 @@ def tile_attend_gds_lch_kernel(tc, xT, wT, vT, wt, xm, offs, out):
             pairs[:].rearrange("p u n e -> p (u n e)").bitcast(U32).rearrange("p (u n) -> p n u", u=2),
         )
         quantize_g(3)
-        middle = gradient(0, PIECE, 3 * PIECE, "pairs")
-        xm_rest = sb.tile([P, 2 * P * PACK], BF16, name="xm_rest", tag="last_slopes", align_bytes=64)
+        late = sb.tile([P, HALF + P * PACK], F32, name="late", tag="pairs", align_bytes=64)
+        middle = gradient(0, PIECE, 3 * PIECE, late[:, :HALF])
+        xm_rest = late[:, HALF:].bitcast(BF16)
         xm_grouped.extend([xm_rest[:, : P * PACK], xm_rest[:, P * PACK :]])
         group_xm(2)
         group_xm(3)
         place(0, PIECE, 3 * PIECE, middle)
-        quantize_xm(2, xm_rest[:])
+        quantize_xm(2, xm_rest)
 
-        for u, first in ((1, HALF), (0, 3 * PIECE), (2, 0), (3, 0)):
+        for u, first in ((0, 3 * PIECE), (1, HALF), (2, 0), (3, 0)):
             place(u, first, N, gradient(u, first, N))
             nc.sync.dma_start(out[u * P : (u + 1) * P, :], windows[u][:])

@@ -101,8 +101,8 @@ def tile_attend_gds_lch_kernel(tc, xT, wT, vT, wt, xm, offs, out):
         def v_half(h):
             return v_grouped[:, :, 1 - h, :, :]
 
-        v_mx = [mx_tiles("v%d" % q, PIECE) for q in range(PIECES)]
-        slopes = [sb.tile([P, PIECE, PACK], F32, name="slopes%d" % q) for q in range(PIECES - 1)]
+        v_mx = [mx_tiles("v%d" % q, PIECE) for q in range(PIECES - 1)]
+        slopes = {}
         g_grouped = [
             sb.tile([P, PIECE, PACK], BF16, name="g_grouped%d" % q, tag="g_grouped%d" % q, align_bytes=64)
             for q in range(PIECES)
@@ -158,8 +158,12 @@ def tile_attend_gds_lch_kernel(tc, xT, wT, vT, wt, xm, offs, out):
 
         def slopes_of(q, cuts):
             for cut in cuts:
+                name = "slopes%d_%d" % (q, cut.start)
+                slopes[q, cut.start] = sb.tile(
+                    [P, cut.stop - cut.start, PACK], F32, name=name, tag=name, align_bytes=64
+                )
                 nc.scalar.activation(
-                    slopes[q][:, cut, :], scores[q][:, :, cut].rearrange("p t n -> p n t"), ACT.Tanh, scale=-1.0
+                    slopes[q, cut.start][:], scores[q][:, :, cut].rearrange("p t n -> p n t"), ACT.Tanh, scale=-1.0
                 )
 
         whole = [slice(0, PIECE)]
@@ -173,7 +177,7 @@ def tile_attend_gds_lch_kernel(tc, xT, wT, vT, wt, xm, offs, out):
         xm_grouped.append(xm_first[:])
         group_xm(0)
         finish_scores(0, in_two)
-        finish_scores(1, in_two)
+        finish_scores(1, whole)
         xm_second = sb.tile([P, P * PACK], BF16, name="xm_second", tag="v1_codes", align_bytes=64)
         xm_grouped.append(xm_second[:])
         group_xm(1)
@@ -182,12 +186,11 @@ def tile_attend_gds_lch_kernel(tc, xT, wT, vT, wt, xm, offs, out):
         )
         quantize_xm(0, xm_grouped[0])
         finish_scores(2, whole)
-        finish_scores(3, [])
 
         def weigh(q, cuts):
             for cut in cuts:
                 weights_wide = row_weights[:].unsqueeze(1).to_broadcast([P, cut.stop - cut.start, PACK])
-                nc.vector.tensor_tensor(g_grouped[q][:, cut, :], slopes[q][:, cut, :], weights_wide, MULT)
+                nc.vector.tensor_tensor(g_grouped[q][:, cut, :], slopes[q, cut.start][:], weights_wide, MULT)
 
         def quantize_g(q):
             slots = slice(PAD + q * PIECE, PAD + (q + 1) * PIECE)
@@ -220,9 +223,11 @@ def tile_attend_gds_lch_kernel(tc, xT, wT, vT, wt, xm, offs, out):
                 nc.vector.tensor_copy(window, staged)
 
         weigh(0, in_two)
-        weigh(1, in_two[:1])
+        last_codes = sb.tile([P, PIECE], U32, name="last_codes", tag="slopes0_0", align_bytes=64)
+        v_mx.append((last_codes, sb.tile([P, PIECE], U8, name="last_scales", align_bytes=64)))
+        finish_scores(3, [])
         quantize_g(0)
-        weigh(1, in_two[1:])
+        weigh(1, whole)
         first_quarter = gradient(0, 0, PIECE)
         last_slopes = sb.tile([P, PACK, PIECE], F32, name="last_slopes", tag="last_slopes", align_bytes=64)
         nc.scalar.activation(last_slopes[:], scores[3][:], ACT.Tanh, scale=-1.0)

@@ -39,6 +39,7 @@ def tile_attend_gds_lch_kernel(tc, xT, wT, vT, wt, xm, offs, out):
         offsets = sb.tile([P, N // 16], U16, name="offsets")
 
         row_weights = sb.tile([P, PACK], F32, name="row_weights")
+        nc.scalar.dma_start(row_weights[:], wt[0].rearrange("(p t) o -> p (t o)", t=PACK))
 
         w_raw = sb.tile([P, PACK, T], F32, name="w_raw")
         nc.sync.dma_start(w_raw[:], wT.rearrange("(p j) c -> p j c", j=PACK))
@@ -56,8 +57,6 @@ def tile_attend_gds_lch_kernel(tc, xT, wT, vT, wt, xm, offs, out):
             piece = sb.tile([P, PACK, (end - first) * P], F32, name="xm_raw%d" % first)
             nc.sync.dma_start(piece[:], xm_rows[:, :, first * P : end * P])
             xm_raw.extend(piece[:, :, u * P : (u + 1) * P] for u in range(end - first))
-            if first == 0:
-                nc.sync.dma_start(row_weights[:], wt[0].rearrange("(p t) o -> p (t o)", t=PACK))
 
         windows = [sb.tile([P, T], F32, name="window%d" % u) for u in range(D // P)]
         for window in windows:

@@ -42,8 +42,8 @@ def tile_attend_gds_lch_kernel(tc, xT, wT, vT, wt, xm, offs, out):
         nc.scalar.dma_start(row_weights[:], wt[0].rearrange("(p t) o -> p (t o)", t=PACK))
 
         w_raw = sb.tile([P, PACK, T], F32, name="w_raw")
-        nc.sync.dma_start(w_raw[:], wT.rearrange("(p j) c -> p j c", j=PACK))
         nc.sync.dma_start(offsets[:], offs)
+        nc.sync.dma_start(w_raw[:], wT.rearrange("(p j) c -> p j c", j=PACK))
         x_raw = sb.tile([P, PACK, R], F32, name="x_raw", tag="x_raw", align_bytes=64)
         nc.sync.dma_start(x_raw[:], xT[0].rearrange("(p j) r -> p j r", j=PACK))
         w_planes = [w_raw[:, j, :] for j in range(PACK)]

@@ -39,14 +39,16 @@ def tile_attend_gds_lch_kernel(tc, xT, wT, vT, wt, xm, offs, out):
         offsets = sb.tile([P, N // 16], U16, name="offsets")
 
         row_weights = sb.tile([P, PACK], F32, name="row_weights")
-        nc.scalar.dma_start(row_weights[:], wt[0].rearrange("(p t) o -> p (t o)", t=PACK))
 
-        w_raw = sb.tile([P, PACK, T], F32, name="w_raw")
+        w_pairs = [sb.tile([P, 2, T], F32, name="w_pair%d" % h) for h in range(2)]
+        w_rows = wT.rearrange("(p j) c -> p j c", j=PACK)
         nc.sync.dma_start(offsets[:], offs)
-        nc.sync.dma_start(w_raw[:], wT.rearrange("(p j) c -> p j c", j=PACK))
+        nc.scalar.dma_start(w_pairs[0][:], w_rows[:, 0:2, :])
+        nc.scalar.dma_start(row_weights[:], wt[0].rearrange("(p t) o -> p (t o)", t=PACK))
+        nc.sync.dma_start(w_pairs[1][:], w_rows[:, 2:4, :])
         x_raw = sb.tile([P, PACK, R], F32, name="x_raw", tag="x_raw", align_bytes=64)
         nc.sync.dma_start(x_raw[:], xT[0].rearrange("(p j) r -> p j r", j=PACK))
-        w_planes = [w_raw[:, j, :] for j in range(PACK)]
+        w_planes = [w_pairs[j // 2][:, j % 2, :] for j in range(PACK)]
         v_planes = [sb.tile([P, T], F32, name="v_plane%d" % j) for j in range(PACK)]
         v_rows = vT.rearrange("(p j) c -> p j c", j=PACK)
         for j in range(PACK):

@@ -14,15 +14,12 @@ E4M3 = mybir.dt.float8_e4m3fn_x4
 E5M2 = mybir.dt.float8_e5m2_x4
 ACT = mybir.ActivationFunctionType
 MULT = mybir.AluOpType.mult
-ADD = mybir.AluOpType.add
 
 P = 128
 PACK = 4
-HALVES = 2
-HALF = N // HALVES
+HALF = N // 2
 PIECES = 4
 PIECE = N // PIECES
-PAD = N - PIECE
 
 
 def tile_attend_gds_lch_kernel(tc, xT, wT, vT, wt, xm, offs, out):
@@ -31,62 +28,75 @@ def tile_attend_gds_lch_kernel(tc, xT, wT, vT, wt, xm, offs, out):
         sb = ctx.enter_context(tc.tile_pool(name="sb", bufs=1))
         psum = ctx.enter_context(tc.psum_pool(name="psum", bufs=1))
 
-        def mx_tiles(name, width):
-            codes = sb.tile([P, width], U32, name=name + "_codes", tag=name + "_codes", align_bytes=64)
-            scales = sb.tile([P, width], U8, name=name + "_scales", align_bytes=64)
-            return codes, scales
+        def tile(name, shape, dtype, tag=None):
+            return sb.tile(shape, dtype, name=name, tag=tag or name, align_bytes=64)
+
+        def mx_tiles(name, width, tag=None):
+            return tile(name + "_codes", [P, width], U32, tag), tile(name + "_scales", [P, width], U8)
+
+        def listed(window, first, end):
+            return window.indirect(offsets[:, first // 16 : end // 16])
 
         offsets = sb.tile([P, N // 16], U16, name="offsets")
-
-        row_weights = sb.tile([P, PACK], F32, name="row_weights")
-
-        w_pairs = [sb.tile([P, 2, T], F32, name="w_pair%d" % h) for h in range(2)]
+        row_weights = tile("row_weights", [P, PACK], F32)
+        w_pairs = [tile("w_pair%d" % h, [P, 2, T], F32) for h in range(2)]
         w_rows = wT.rearrange("(p j) c -> p j c", j=PACK)
         nc.sync.dma_start(offsets[:], offs)
         nc.scalar.dma_start(w_pairs[0][:], w_rows[:, 0:2, :])
         nc.scalar.dma_start(row_weights[:], wt[0].rearrange("(p t) o -> p (t o)", t=PACK))
         nc.sync.dma_start(w_pairs[1][:], w_rows[:, 2:4, :])
-        x_raw = sb.tile([P, PACK, R], F32, name="x_raw", tag="x_raw", align_bytes=64)
+        x_raw = tile("x_raw", [P, PACK, R], F32)
         nc.sync.dma_start(x_raw[:], xT[0].rearrange("(p j) r -> p j r", j=PACK))
-        w_planes = [w_pairs[j // 2][:, j % 2, :] for j in range(PACK)]
-        v_planes = [sb.tile([P, T], F32, name="v_plane%d" % j) for j in range(PACK)]
+        v_planes = [tile("v_plane%d" % j, [P, T], F32) for j in range(PACK)]
         v_rows = vT.rearrange("(p j) c -> p j c", j=PACK)
         for j in range(PACK):
             nc.sync.dma_start(v_planes[j][:], v_rows[:, j, :])
         xm_rows = xm[0].rearrange("(p t) d -> p t d", t=PACK)
         xm_raw = []
         for first, end in ((0, 1), (1, 2), (2, 4)):
-            piece = sb.tile([P, PACK, (end - first) * P], F32, name="xm_raw%d" % first)
+            piece = tile("xm_raw%d" % first, [P, PACK, (end - first) * P], F32)
             nc.sync.dma_start(piece[:], xm_rows[:, :, first * P : end * P])
-            xm_raw.extend(piece[:, :, u * P : (u + 1) * P] for u in range(end - first))
+            xm_raw.append(piece)
 
-        windows = [sb.tile([P, T], F32, name="window%d" % u) for u in range(D // P)]
+        windows = [tile("window%d" % u, [P, T], F32) for u in range(D // P)]
         for window in windows:
             nc.gpsimd.memset(window[:], 0.0)
+        ones = tile("ones", [P, 1], F32)
+        nc.gpsimd.memset(ones[:], 1.0)
 
-        x_grouped = sb.tile([P, R * PACK], BF16, name="x_grouped", align_bytes=64)
-        nc.scalar.copy(
-            x_grouped[:].rearrange("p (t m j) -> p m j t", t=PACK, j=PACK),
-            x_raw[:].rearrange("p j (m t) -> p m j t", t=PACK),
-        )
-        x_codes, x_scales = mx_tiles("x", R)
-        nc.vector.quantize_mx(x_codes[:].bitcast(E4M3), x_scales[:], x_grouped[:])
-
-        w_picked = sb.tile([P, PACK, N], F32, name="w_picked")
-        for j in range(PACK):
-            nc.vector.tensor_copy(w_picked[:, j, :], w_planes[j].indirect(offsets[:]))
-        w_grouped = sb.tile([P, N * PACK], BF16, name="w_grouped", tag="x_raw", align_bytes=64)
+        w_picked = tile("w_picked", [P, PACK, N], F32)
+        for j in range(2):
+            nc.scalar.activation(w_picked[:, j, :], listed(w_pairs[0][:, j, :], 0, N), ACT.Copy)
+            nc.vector.tensor_copy(w_picked[:, 2 + j, :], listed(w_pairs[1][:, j, :], 0, N))
+        w_grouped = tile("w_grouped", [P, N * PACK], BF16)
         nc.scalar.activation(
             w_grouped[:].rearrange("p (c i j) -> p c j i", i=4, j=PACK),
             w_picked[:].rearrange("p j (c i) -> p c j i", i=4),
             ACT.Copy,
             scale=-1.0,
         )
+        x_grouped = tile("x_grouped", [P, R * PACK], BF16)
+        nc.vector.tensor_copy(
+            x_grouped[:].rearrange("p (t m j) -> p m j t", t=PACK, j=PACK),
+            x_raw[:].rearrange("p j (m t) -> p m j t", t=PACK),
+        )
+        x_rest = mx_tiles("x_rest", R - P)
+        nc.vector.quantize_mx(x_rest[0][:].bitcast(E4M3), x_rest[1][:], x_grouped[:, P * PACK :])
+
+        v_grouped = tile("v_grouped", [P, N, PACK], BF16)
+        nc.vector.tensor_copy(v_grouped[:, :, 0], listed(v_planes[0][:], 0, N))
+        w_codes, w_scales = mx_tiles("w", N)
+        nc.vector.quantize_mx(w_codes[:].bitcast(E4M3), w_scales[:], w_grouped[:])
+        nc.vector.tensor_copy(v_grouped[:, :, 1], listed(v_planes[1][:], 0, N))
+        x_first = mx_tiles("x_first", P, "v_plane1")
+        nc.vector.quantize_mx(x_first[0][:].bitcast(E4M3), x_first[1][:], x_grouped[:, : P * PACK])
+
         scores = [psum.tile([P, PACK, PIECE], F32, name="scores%d" % q) for q in range(PIECES)]
 
         def score_passes(q, codes, scales, opens):
             for t in range(PACK):
-                rows = slice(t * P, (t + 1) * P)
+                x_codes, x_scales = x_rest if t else x_first
+                rows = slice((t - 1) * P, t * P) if t else slice(0, P)
                 nc.tensor.matmul_mx(
                     scores[q][:, t, :],
                     lhsT=x_codes[:, rows].bitcast(E4M3),
@@ -97,167 +107,102 @@ def tile_attend_gds_lch_kernel(tc, xT, wT, vT, wt, xm, offs, out):
                     stop=(not opens and t == PACK - 1),
                 )
 
-        v_grouped = sb.tile([P, HALVES, HALVES, PIECE, PACK], BF16, name="v_grouped", align_bytes=64)
-
-        def v_half(h):
-            return v_grouped[:, :, 1 - h, :, :]
-
-        v_mx = [mx_tiles("v%d" % q, PIECE) for q in range(PIECES - 1)]
-        slopes = {}
-        g_grouped = [
-            sb.tile([P, PIECE, PACK], BF16, name="g_grouped%d" % q, tag="g_grouped%d" % q, align_bytes=64)
-            for q in range(PIECES)
-        ]
-        g_codes, g_scales = mx_tiles("g", PAD + N)
-        nc.gpsimd.memset(g_codes[:, :PAD], 0)
-        nc.gpsimd.memset(g_scales[:, :PAD], 127)
-        zeros = sb.tile([P, PIECE], F32, name="zeros")
-        nc.gpsimd.memset(zeros[:], 0.0)
-        xm_codes, xm_scales = mx_tiles("xm", D)
-        xm_grouped = []
-
-        def group_xm(u):
-            nc.scalar.copy(
-                xm_grouped[u].rearrange("p (c i t) -> p c t i", i=4, t=PACK),
-                xm_raw[u].rearrange("p t (c i) -> p c t i", i=4),
-            )
-
-        def quantize_xm(u, grouped):
-            cols = slice(u * P, u * P + grouped.shape[1] // PACK)
-            nc.vector.quantize_mx(xm_codes[:, cols].bitcast(E4M3), xm_scales[:, cols], grouped)
-
-        v_early = [
-            sb.tile([P, 2, HALF], F32, name="v_early%d" % h, tag="v_early%d" % h, align_bytes=64) for h in range(HALVES)
-        ]
-        for j in range(2):
-            for h in range(HALVES):
-                nc.vector.tensor_copy(
-                    v_early[h][:, j, :], v_planes[j][:].indirect(offsets[:, h * HALF // 16 : (h + 1) * HALF // 16])
-                )
-        for h in range(HALVES):
-            nc.scalar.copy(v_half(h)[:, :, :, 0:2], v_early[h][:].rearrange("p j (k n) -> p k n j", k=HALVES))
-        w_codes = sb.tile([P, N], U32, name="w_codes", tag="v_early0", align_bytes=64)
-        w_scales = sb.tile([P, N], U8, name="w_scales", align_bytes=64)
-        nc.vector.quantize_mx(w_codes[:].bitcast(E4M3), w_scales[:], w_grouped[:])
         for q in range(PIECES):
             slots = slice(q * PIECE, (q + 1) * PIECE)
             score_passes(q, w_codes[:, slots], w_scales[:, slots], True)
-        v_late = sb.tile([P, 2, N], BF16, name="v_late")
-        nc.vector.tensor_copy(v_late[:, 0, :], v_planes[2][:].indirect(offsets[:]))
-        for first, end in ((0, PIECE), (PIECE, HALF), (HALF, N)):
-            nc.vector.tensor_copy(v_late[:, 1, first:end], v_planes[3][:].indirect(offsets[:, first // 16 : end // 16]))
 
-        def finish_scores(q, cuts):
-            v_codes, v_scales = v_mx[q]
+        for j in (2, 3):
+            for q in range(2):
+                first, end = q * PIECE, (q + 1) * PIECE
+                nc.scalar.activation(v_grouped[:, first:end, j], listed(v_planes[j][:], first, end), ACT.Copy)
+            nc.vector.tensor_copy(v_grouped[:, HALF:, j], listed(v_planes[j][:], HALF, N))
+
+        xm_codes, xm_scales = mx_tiles("xm", D)
+
+        def group_xm(copy, grouped, raw):
+            copy(
+                grouped[:].rearrange("p (c i t) -> p c t i", i=4, t=PACK),
+                raw[:].rearrange("p t (c i) -> p c t i", i=4),
+            )
+
+        def quantize_xm(first, grouped):
+            cols = slice(first * P, first * P + grouped.shape[1] // PACK)
+            nc.vector.quantize_mx(xm_codes[:, cols].bitcast(E4M3), xm_scales[:, cols], grouped[:])
+
+        xm_first = tile("xm_first", [P, P * PACK], BF16)
+        group_xm(nc.scalar.copy, xm_first, xm_raw[0])
+        slopes = []
+        for q in range(PIECES):
+            v_codes, v_scales = mx_tiles("v%d" % q, PIECE)
             nc.vector.quantize_mx(
                 v_codes[:].bitcast(E4M3),
                 v_scales[:],
-                v_half(q // 2)[:, q % 2, :, :].rearrange("p n j -> p (n j)"),
+                v_grouped[:, q * PIECE : (q + 1) * PIECE, :].rearrange("p n j -> p (n j)"),
             )
             score_passes(q, v_codes[:], v_scales[:], False)
-            slopes_of(q, cuts)
+            slopes.append(tile("slopes%d" % q, [P, PIECE, PACK], F32))
+            nc.scalar.activation(slopes[q][:], scores[q][:].rearrange("p t n -> p n t"), ACT.Tanh, scale=-1.0)
+        xm_second = tile("xm_second", [P, P * PACK], BF16)
+        group_xm(nc.vector.tensor_copy, xm_second, xm_raw[1])
+        quantize_xm(0, xm_first)
+        quantize_xm(1, xm_second)
 
-        def slopes_of(q, cuts):
-            for cut in cuts:
-                name = "slopes%d_%d" % (q, cut.start)
-                slopes[q, cut.start] = sb.tile(
-                    [P, cut.stop - cut.start, PACK], F32, name=name, tag=name, align_bytes=64
-                )
-                nc.scalar.activation(
-                    slopes[q, cut.start][:], scores[q][:, :, cut].rearrange("p t n -> p n t"), ACT.Tanh, scale=-1.0
-                )
+        g_codes, g_scales = mx_tiles("g", N)
+        weights_wide = row_weights[:].unsqueeze(1).to_broadcast([P, PIECE, PACK])
 
-        whole = [slice(0, PIECE)]
-        in_two = [slice(0, PIECE // 2), slice(PIECE // 2, PIECE)]
+        def weigh(q):
+            grouped = tile("g_grouped%d" % q, [P, PIECE, PACK], BF16, "g_grouped%d" % (q % 2 if q == 2 else q))
+            nc.vector.tensor_tensor(grouped[:], slopes[q][:], weights_wide, MULT)
+            return grouped
 
-        for q in range(2):
-            nc.scalar.copy(
-                v_half(0)[:, q, :, 2:4], v_late[:, :, q * PIECE : (q + 1) * PIECE].rearrange("p j n -> p n j")
-            )
-        xm_first = sb.tile([P, P * PACK], BF16, name="xm_first", align_bytes=64)
-        xm_grouped.append(xm_first[:])
-        group_xm(0)
-        finish_scores(0, in_two)
-        finish_scores(1, whole)
-        xm_second = sb.tile([P, P * PACK], BF16, name="xm_second", tag="v1_codes", align_bytes=64)
-        xm_grouped.append(xm_second[:])
-        group_xm(1)
-        nc.vector.tensor_copy(
-            v_half(1)[:, :, :, 2:4], v_late[:, :, HALF:].rearrange("p j (k n) -> p k n j", k=HALVES)
-        )
-        quantize_xm(0, xm_grouped[0])
-        finish_scores(2, whole)
-
-        def weigh(q, cuts):
-            for cut in cuts:
-                weights_wide = row_weights[:].unsqueeze(1).to_broadcast([P, cut.stop - cut.start, PACK])
-                nc.vector.tensor_tensor(g_grouped[q][:, cut, :], slopes[q, cut.start][:], weights_wide, MULT)
-
-        def quantize_g(q):
-            slots = slice(PAD + q * PIECE, PAD + (q + 1) * PIECE)
+        def quantize_g(q, grouped):
+            slots = slice(q * PIECE, (q + 1) * PIECE)
             nc.vector.quantize_mx(
-                g_codes[:, slots].bitcast(E5M2), g_scales[:, slots], g_grouped[q][:].rearrange("p n t -> p (n t)")
+                g_codes[:, slots].bitcast(E5M2), g_scales[:, slots], grouped[:].rearrange("p n t -> p (n t)")
             )
 
-        def gradient(u, first, end, staged=None):
-            grads = psum.tile([P, N], F32, name="grads%d_%d" % (u, end), tag="grads", bufs=4)
-            words = slice(PAD + end - N, PAD + end)
+        def gradient(u, first, end):
+            grads = psum.tile([P, end - first], F32, name="grads%d_%d" % (u, end), tag="grads", bufs=4)
             nc.tensor.matmul_mx(
                 grads[:],
                 lhsT=xm_codes[:, u * P : (u + 1) * P].bitcast(E4M3),
                 lhsT_scale=xm_scales[:, u * P : (u + 1) * P],
-                rhs=g_codes[:, words].bitcast(E5M2),
-                rhs_scale=g_scales[:, words],
+                rhs=g_codes[:, first:end].bitcast(E5M2),
+                rhs_scale=g_scales[:, first:end],
                 start=True,
                 stop=True,
             )
-            if staged is None:
-                staged = sb.tile([P, end - first], F32, name="staged%d_%d" % (u, end))[:]
-            nc.scalar.copy(staged, grads[:, N - (end - first) :])
+            return grads
+
+        def staged_by(copy, name, grads):
+            staged = tile(name, list(grads.shape), F32)
+            copy(staged[:], grads[:])
             return staged
 
-        def place(u, first, end, staged):
-            window = windows[u][:].indirect(offsets[:, first // 16 : end // 16])
-            if end - first == PIECE:
-                nc.vector.tensor_tensor(window, staged, zeros[:], ADD)
-            else:
-                nc.vector.tensor_copy(window, staged)
-
-        weigh(0, in_two)
-        last_codes = sb.tile([P, PIECE], U32, name="last_codes", tag="slopes0_0", align_bytes=64)
-        v_mx.append((last_codes, sb.tile([P, PIECE], U8, name="last_scales", align_bytes=64)))
-        finish_scores(3, [])
-        quantize_g(0)
-        weigh(1, whole)
-        first_quarter = gradient(0, 0, PIECE)
-        last_slopes = sb.tile([P, PACK, PIECE], F32, name="last_slopes", tag="last_slopes", align_bytes=64)
-        nc.scalar.activation(last_slopes[:], scores[3][:], ACT.Tanh, scale=-1.0)
-        quantize_xm(1, xm_grouped[1])
-        quantize_g(1)
-        first_half = gradient(1, 0, HALF)
-        weigh(2, whole)
-        place(0, 0, PIECE, first_quarter)
-        quantize_g(2)
-        place(1, 0, HALF, first_half)
-        pairs = sb.tile([P, 2, PIECE, 2], BF16, name="pairs", tag="pairs", align_bytes=64)
-        for t in range(PACK):
-            nc.scalar.activation(
-                pairs[:, t // 2, :, t % 2], last_slopes[:, t, :], ACT.Copy, scale=row_weights[:, t : t + 1]
-            )
-        nc.scalar.copy(
-            g_grouped[3][:].rearrange("p n t -> p (n t)").bitcast(U32).rearrange("p (n u) -> p n u", u=2),
-            pairs[:].rearrange("p u n e -> p (u n e)").bitcast(U32).rearrange("p (u n) -> p n u", u=2),
-        )
-        quantize_g(3)
-        late = sb.tile([P, HALF + P * PACK], F32, name="late", tag="pairs", align_bytes=64)
-        middle = gradient(0, PIECE, 3 * PIECE, late[:, :HALF])
-        xm_rest = late[:, HALF:].bitcast(BF16)
-        xm_grouped.extend([xm_rest[:, : P * PACK], xm_rest[:, P * PACK :]])
-        group_xm(2)
-        group_xm(3)
-        place(0, PIECE, 3 * PIECE, middle)
-        quantize_xm(2, xm_rest)
-
-        for u, first in ((0, 3 * PIECE), (1, HALF), (2, 0), (3, 0)):
-            place(u, first, N, gradient(u, first, N))
+        def store(u):
             nc.sync.dma_start(out[u * P : (u + 1) * P, :], windows[u][:])
+
+        for pair in range(2):
+            grouped = [weigh(2 * pair), weigh(2 * pair + 1)]
+            quantize_g(2 * pair, grouped[0])
+            quantize_g(2 * pair + 1, grouped[1])
+            if pair == 0:
+                early = staged_by(nc.scalar.copy, "early", gradient(0, 0, HALF))
+                nc.scalar.activation(listed(windows[0][:], 0, HALF), early[:], ACT.Copy)
+        grads_late = gradient(0, HALF, N)
+        grads_one = gradient(1, 0, N)
+        xm_rest = tile("xm_rest", [P, 2 * P * PACK], BF16, "slopes3")
+        group_xm(nc.vector.tensor_copy, xm_rest, xm_raw[2])
+        late = staged_by(nc.vector.tensor_copy, "late", grads_late)
+        one = staged_by(nc.vector.tensor_copy, "one", grads_one)
+        nc.scalar.activation(listed(windows[0][:], HALF, N), late[:], ACT.Copy)
+        store(0)
+        quantize_xm(2, xm_rest)
+        nc.vector.tensor_copy(listed(windows[1][:], 0, N), one[:])
+        store(1)
+        two = staged_by(nc.scalar.copy, "two", gradient(2, 0, N))
+        three = staged_by(nc.scalar.copy, "three", gradient(3, 0, N))
+        nc.scalar.activation(listed(windows[2][:], 0, N), two[:], ACT.Copy, scale=ones[:])
+        store(2)
+        nc.vector.tensor_copy(listed(windows[3][:], 0, N), three[:])
+        store(3)

@@ -53,7 +53,7 @@ def tile_attend_gds_lch_kernel(tc, xT, wT, vT, wt, xm, offs, out):
             nc.sync.dma_start(v_planes[j][:], v_rows[:, j, :])
         xm_rows = xm[0].rearrange("(p t) d -> p t d", t=PACK)
         xm_raw = []
-        for first, end in ((0, 1), (1, 2), (2, 4)):
+        for first, end in ((0, 1), (1, 4)):
             piece = tile("xm_raw%d" % first, [P, PACK, (end - first) * P], F32)
             nc.sync.dma_start(piece[:], xm_rows[:, :, first * P : end * P])
             xm_raw.append(piece)
@@ -117,21 +117,25 @@ def tile_attend_gds_lch_kernel(tc, xT, wT, vT, wt, xm, offs, out):
                 nc.scalar.activation(v_grouped[:, first:end, j], listed(v_planes[j][:], first, end), ACT.Copy)
             nc.vector.tensor_copy(v_grouped[:, HALF:, j], listed(v_planes[j][:], HALF, N))
 
-        xm_codes, xm_scales = mx_tiles("xm", D)
+        xm_mx = {}
 
         def group_xm(copy, grouped, raw):
             copy(
-                grouped[:].rearrange("p (c i t) -> p c t i", i=4, t=PACK),
-                raw[:].rearrange("p t (c i) -> p c t i", i=4),
+                grouped.rearrange("p (c i t) -> p c t i", i=4, t=PACK),
+                raw.rearrange("p t (c i) -> p c t i", i=4),
             )
 
-        def quantize_xm(first, grouped):
-            cols = slice(first * P, first * P + grouped.shape[1] // PACK)
-            nc.vector.quantize_mx(xm_codes[:, cols].bitcast(E4M3), xm_scales[:, cols], grouped[:])
+        def quantize_xm(first, grouped, tag=None):
+            width = grouped.shape[1] // PACK
+            codes, scales = mx_tiles("xm%d" % first, width, tag)
+            nc.vector.quantize_mx(codes[:].bitcast(E4M3), scales[:], grouped)
+            for u in range(width // P):
+                xm_mx[first + u] = codes[:, u * P : (u + 1) * P], scales[:, u * P : (u + 1) * P]
 
         xm_first = tile("xm_first", [P, P * PACK], BF16)
-        group_xm(nc.scalar.copy, xm_first, xm_raw[0])
-        slopes = []
+        group_xm(nc.scalar.copy, xm_first[:], xm_raw[0][:])
+        cuts = [[slice(0, PIECE // 2), slice(PIECE // 2, PIECE)]] * 2 + [[slice(0, PIECE)]] * 2
+        slopes = {}
         for q in range(PIECES):
             v_codes, v_scales = mx_tiles("v%d" % q, PIECE)
             nc.vector.quantize_mx(
@@ -140,69 +144,81 @@ def tile_attend_gds_lch_kernel(tc, xT, wT, vT, wt, xm, offs, out):
                 v_grouped[:, q * PIECE : (q + 1) * PIECE, :].rearrange("p n j -> p (n j)"),
             )
             score_passes(q, v_codes[:], v_scales[:], False)
-            slopes.append(tile("slopes%d" % q, [P, PIECE, PACK], F32))
-            nc.scalar.activation(slopes[q][:], scores[q][:].rearrange("p t n -> p n t"), ACT.Tanh, scale=-1.0)
-        xm_second = tile("xm_second", [P, P * PACK], BF16)
-        group_xm(nc.vector.tensor_copy, xm_second, xm_raw[1])
-        quantize_xm(0, xm_first)
-        quantize_xm(1, xm_second)
+            for c, cut in enumerate(cuts[q]):
+                slopes[q, c] = tile("slopes%d_%d" % (q, c), [P, cut.stop - cut.start, PACK], F32)
+                nc.scalar.activation(
+                    slopes[q, c][:], scores[q][:, :, cut].rearrange("p t n -> p n t"), ACT.Tanh, scale=-1.0
+                )
+        quantize_xm(0, xm_first[:])
 
         g_codes, g_scales = mx_tiles("g", N)
-        weights_wide = row_weights[:].unsqueeze(1).to_broadcast([P, PIECE, PACK])
+        g_grouped = {}
 
-        def weigh(q):
-            grouped = tile("g_grouped%d" % q, [P, PIECE, PACK], BF16, "g_grouped%d" % (q % 2 if q == 2 else q))
-            nc.vector.tensor_tensor(grouped[:], slopes[q][:], weights_wide, MULT)
-            return grouped
+        def weigh(q, c):
+            if c == 0:
+                tag = "slopes1_1" if q == 2 else None
+                g_grouped[q] = tile("g_grouped%d" % q, [P, PIECE, PACK], BF16, tag)
+            cut = cuts[q][c]
+            weights_wide = row_weights[:].unsqueeze(1).to_broadcast([P, cut.stop - cut.start, PACK])
+            nc.vector.tensor_tensor(g_grouped[q][:, cut, :], slopes[q, c][:], weights_wide, MULT)
 
-        def quantize_g(q, grouped):
+        def quantize_g(q):
             slots = slice(q * PIECE, (q + 1) * PIECE)
             nc.vector.quantize_mx(
-                g_codes[:, slots].bitcast(E5M2), g_scales[:, slots], grouped[:].rearrange("p n t -> p (n t)")
+                g_codes[:, slots].bitcast(E5M2), g_scales[:, slots], g_grouped[q][:].rearrange("p n t -> p (n t)")
             )
 
-        def gradient(u, first, end):
-            grads = psum.tile([P, end - first], F32, name="grads%d_%d" % (u, end), tag="grads", bufs=4)
+        staged = [tile("staged%d" % u, [P, N], F32) for u in range(D // P)]
+
+        def gradient(u, first, end, bank):
+            grads = psum.tile([P, end - first], F32, name="grads%d_%d" % (u, first), tag="bank%d" % bank)
+            slots = slice(first, end)
             nc.tensor.matmul_mx(
                 grads[:],
-                lhsT=xm_codes[:, u * P : (u + 1) * P].bitcast(E4M3),
-                lhsT_scale=xm_scales[:, u * P : (u + 1) * P],
-                rhs=g_codes[:, first:end].bitcast(E5M2),
-                rhs_scale=g_scales[:, first:end],
+                lhsT=xm_mx[u][0].bitcast(E4M3),
+                lhsT_scale=xm_mx[u][1],
+                rhs=g_codes[:, slots].bitcast(E5M2),
+                rhs_scale=g_scales[:, slots],
                 start=True,
                 stop=True,
             )
-            return grads
-
-        def staged_by(copy, name, grads):
-            staged = tile(name, list(grads.shape), F32)
-            copy(staged[:], grads[:])
-            return staged
+            return staged[u][:, slots], grads[:]
 
         def store(u):
             nc.sync.dma_start(out[u * P : (u + 1) * P, :], windows[u][:])
 
-        for pair in range(2):
-            grouped = [weigh(2 * pair), weigh(2 * pair + 1)]
-            quantize_g(2 * pair, grouped[0])
-            quantize_g(2 * pair + 1, grouped[1])
-            if pair == 0:
-                early = staged_by(nc.scalar.copy, "early", gradient(0, 0, HALF))
-                nc.scalar.activation(listed(windows[0][:], 0, HALF), early[:], ACT.Copy)
-        grads_late = gradient(0, HALF, N)
-        grads_one = gradient(1, 0, N)
-        xm_rest = tile("xm_rest", [P, 2 * P * PACK], BF16, "slopes3")
-        group_xm(nc.vector.tensor_copy, xm_rest, xm_raw[2])
-        late = staged_by(nc.vector.tensor_copy, "late", grads_late)
-        one = staged_by(nc.vector.tensor_copy, "one", grads_one)
-        nc.scalar.activation(listed(windows[0][:], HALF, N), late[:], ACT.Copy)
+        weigh(0, 0)
+        weigh(0, 1)
+        weigh(1, 0)
+        weigh(1, 1)
+        quantize_g(0)
+        quantize_g(1)
+        xm_second = tile("xm_second", [P, P * PACK], BF16, "slopes1_0")
+        group_xm(nc.scalar.copy, xm_second[:], xm_raw[1][:, :, :P])
+        nc.scalar.copy(*gradient(0, 0, PIECE, 0))
+        nc.scalar.copy(*gradient(0, PIECE, HALF, 1))
+        nc.scalar.activation(listed(windows[0][:], 0, HALF), staged[0][:, :HALF], ACT.Copy)
+        weigh(2, 0)
+        weigh(3, 0)
+        quantize_xm(1, xm_second[:])
+        nc.scalar.copy(*gradient(1, 0, HALF, 0))
+        quantize_g(2)
+        quantize_g(3)
+        late = [gradient(0, HALF, N, 2), gradient(1, HALF, N, 3)]
+        xm_rest = tile("xm_rest", [P, 2 * P * PACK], BF16, "slopes3_0")
+        group_xm(nc.vector.tensor_copy, xm_rest[:], xm_raw[1][:, :, P:])
+        nc.vector.tensor_copy(*late[0])
+        nc.vector.tensor_copy(*late[1])
+        quantize_xm(2, xm_rest[:])
+        nc.scalar.activation(listed(windows[0][:], HALF, N), staged[0][:, HALF:], ACT.Copy)
         store(0)
-        quantize_xm(2, xm_rest)
-        nc.vector.tensor_copy(listed(windows[1][:], 0, N), one[:])
+        nc.vector.tensor_copy(listed(windows[1][:], HALF, N), staged[1][:, HALF:])
+        nc.vector.tensor_copy(*gradient(3, HALF, N, 1))
+        nc.vector.tensor_copy(listed(windows[1][:], 0, HALF), staged[1][:, :HALF])
         store(1)
-        two = staged_by(nc.scalar.copy, "two", gradient(2, 0, N))
-        three = staged_by(nc.scalar.copy, "three", gradient(3, 0, N))
-        nc.scalar.activation(listed(windows[2][:], 0, N), two[:], ACT.Copy, scale=ones[:])
+        nc.scalar.copy(*gradient(2, 0, N, 2))
+        nc.scalar.copy(*gradient(3, 0, HALF, 3))
+        nc.scalar.activation(listed(windows[2][:], 0, N), staged[2][:], ACT.Copy, scale=ones[:])
         store(2)
-        nc.vector.tensor_copy(listed(windows[3][:], 0, N), three[:])
+        nc.vector.tensor_copy(listed(windows[3][:], 0, N), staged[3][:])
         store(3)

@@ -83,13 +83,23 @@ def tile_attend_gds_lch_kernel(tc, xT, wT, vT, wt, xm, offs, out):
         x_rest = mx_tiles("x_rest", R - P)
         nc.vector.quantize_mx(x_rest[0][:].bitcast(E4M3), x_rest[1][:], x_grouped[:, P * PACK :])
 
-        v_grouped = tile("v_grouped", [P, N, PACK], BF16)
-        nc.vector.tensor_copy(v_grouped[:, :, 0], listed(v_planes[0][:], 0, N))
+        v_grouped = tile("v_grouped", [P, 2, 2, PIECE, PACK], BF16)
+
+        def v_half(h):
+            return v_grouped[:, :, 1 - h, :, :]
+
+        def weave(copy, h, first, planes):
+            copy(v_half(h)[:, :, :, first : first + 2], planes.rearrange("p j (k n) -> p k n j", k=2))
+
+        v_early = tile("v_early", [P, 2, N], BF16)
+        nc.vector.tensor_copy(v_early[:, 0, :], listed(v_planes[0][:], 0, N))
         w_codes, w_scales = mx_tiles("w", N)
         nc.vector.quantize_mx(w_codes[:].bitcast(E4M3), w_scales[:], w_grouped[:])
-        nc.vector.tensor_copy(v_grouped[:, :, 1], listed(v_planes[1][:], 0, N))
+        nc.vector.tensor_copy(v_early[:, 1, :], listed(v_planes[1][:], 0, N))
         x_first = mx_tiles("x_first", P, "v_plane1")
         nc.vector.quantize_mx(x_first[0][:].bitcast(E4M3), x_first[1][:], x_grouped[:, : P * PACK])
+        weave(nc.vector.tensor_copy, 0, 0, v_early[:, :, :HALF])
+        weave(nc.scalar.copy, 1, 0, v_early[:, :, HALF:])
 
         scores = [psum.tile([P, PACK, PIECE], F32, name="scores%d" % q) for q in range(PIECES)]
 
@@ -111,11 +121,12 @@ def tile_attend_gds_lch_kernel(tc, xT, wT, vT, wt, xm, offs, out):
             slots = slice(q * PIECE, (q + 1) * PIECE)
             score_passes(q, w_codes[:, slots], w_scales[:, slots], True)
 
+        v_late = tile("v_late", [P, 2, HALF], BF16)
         for j in (2, 3):
             for q in range(2):
                 first, end = q * PIECE, (q + 1) * PIECE
-                nc.scalar.activation(v_grouped[:, first:end, j], listed(v_planes[j][:], first, end), ACT.Copy)
-            nc.vector.tensor_copy(v_grouped[:, HALF:, j], listed(v_planes[j][:], HALF, N))
+                nc.scalar.activation(v_half(0)[:, q, :, j], listed(v_planes[j][:], first, end), ACT.Copy)
+            nc.vector.tensor_copy(v_late[:, j - 2, :], listed(v_planes[j][:], HALF, N))
 
         xm_mx = {}
 
@@ -141,9 +152,11 @@ def tile_attend_gds_lch_kernel(tc, xT, wT, vT, wt, xm, offs, out):
             nc.vector.quantize_mx(
                 v_codes[:].bitcast(E4M3),
                 v_scales[:],
-                v_grouped[:, q * PIECE : (q + 1) * PIECE, :].rearrange("p n j -> p (n j)"),
+                v_half(q // 2)[:, q % 2, :, :].rearrange("p n j -> p (n j)"),
             )
             score_passes(q, v_codes[:], v_scales[:], False)
+            if q == 1:
+                weave(nc.vector.tensor_copy, 1, 2, v_late[:])
             for c, cut in enumerate(cuts[q]):
                 slopes[q, c] = tile("slopes%d_%d" % (q, c), [P, cut.stop - cut.start, PACK], F32)
                 nc.scalar.activation(

@@ -53,7 +53,7 @@ def tile_attend_gds_lch_kernel(tc, xT, wT, vT, wt, xm, offs, out):
             nc.sync.dma_start(v_planes[j][:], v_rows[:, j, :])
         xm_rows = xm[0].rearrange("(p t) d -> p t d", t=PACK)
         xm_raw = []
-        for first, end in ((0, 1), (1, 4)):
+        for first, end in ((0, 1), (1, 2), (2, 4)):
             piece = tile("xm_raw%d" % first, [P, PACK, (end - first) * P], F32)
             nc.sync.dma_start(piece[:], xm_rows[:, :, first * P : end * P])
             xm_raw.append(piece)
@@ -83,14 +83,7 @@ def tile_attend_gds_lch_kernel(tc, xT, wT, vT, wt, xm, offs, out):
         x_rest = mx_tiles("x_rest", R - P)
         nc.vector.quantize_mx(x_rest[0][:].bitcast(E4M3), x_rest[1][:], x_grouped[:, P * PACK :])
 
-        v_grouped = tile("v_grouped", [P, 2, 2, PIECE, PACK], BF16)
-
-        def v_half(h):
-            return v_grouped[:, :, 1 - h, :, :]
-
-        def weave(copy, h, first, planes):
-            copy(v_half(h)[:, :, :, first : first + 2], planes.rearrange("p j (k n) -> p k n j", k=2))
-
+        v_grouped = tile("v_grouped", [P, N, PACK], BF16)
         v_early = tile("v_early", [P, 2, N], BF16)
         nc.vector.tensor_copy(v_early[:, 0, :], listed(v_planes[0][:], 0, N))
         w_codes, w_scales = mx_tiles("w", N)
@@ -98,10 +91,9 @@ def tile_attend_gds_lch_kernel(tc, xT, wT, vT, wt, xm, offs, out):
         nc.vector.tensor_copy(v_early[:, 1, :], listed(v_planes[1][:], 0, N))
         x_first = mx_tiles("x_first", P, "v_plane1")
         nc.vector.quantize_mx(x_first[0][:].bitcast(E4M3), x_first[1][:], x_grouped[:, : P * PACK])
-        weave(nc.vector.tensor_copy, 0, 0, v_early[:, :, :HALF])
-        weave(nc.scalar.copy, 1, 0, v_early[:, :, HALF:])
+        nc.vector.tensor_copy(v_grouped[:, :, 0:2], v_early[:].rearrange("p j n -> p n j"))
 
-        scores = [psum.tile([P, PACK, PIECE], F32, name="scores%d" % q) for q in range(PIECES)]
+        scores = [psum.tile([P, PACK, PIECE], F32, name="scores%d" % q, tag="scores%d" % q) for q in range(PIECES)]
 
         def score_passes(q, codes, scales, opens):
             for t in range(PACK):
@@ -121,12 +113,10 @@ def tile_attend_gds_lch_kernel(tc, xT, wT, vT, wt, xm, offs, out):
             slots = slice(q * PIECE, (q + 1) * PIECE)
             score_passes(q, w_codes[:, slots], w_scales[:, slots], True)
 
-        v_late = tile("v_late", [P, 2, HALF], BF16)
-        for j in (2, 3):
-            for q in range(2):
-                first, end = q * PIECE, (q + 1) * PIECE
-                nc.scalar.activation(v_half(0)[:, q, :, j], listed(v_planes[j][:], first, end), ACT.Copy)
-            nc.vector.tensor_copy(v_late[:, j - 2, :], listed(v_planes[j][:], HALF, N))
+        nc.scalar.activation(v_grouped[:, :, 2], listed(v_planes[2][:], 0, N), ACT.Copy)
+        for first in range(0, N, PIECE):
+            end = first + PIECE
+            nc.scalar.activation(v_grouped[:, first:end, 3], listed(v_planes[3][:], first, end), ACT.Copy)
 
         xm_mx = {}
 
@@ -143,8 +133,7 @@ def tile_attend_gds_lch_kernel(tc, xT, wT, vT, wt, xm, offs, out):
             for u in range(width // P):
                 xm_mx[first + u] = codes[:, u * P : (u + 1) * P], scales[:, u * P : (u + 1) * P]
 
-        xm_first = tile("xm_first", [P, P * PACK], BF16)
-        group_xm(nc.scalar.copy, xm_first[:], xm_raw[0][:])
+        xm_early = [tile("xm_early%d" % u, [P, P * PACK], BF16) for u in range(2)]
         cuts = [[slice(0, PIECE // 2), slice(PIECE // 2, PIECE)]] * 2 + [[slice(0, PIECE)]] * 2
         slopes = {}
         for q in range(PIECES):
@@ -152,17 +141,18 @@ def tile_attend_gds_lch_kernel(tc, xT, wT, vT, wt, xm, offs, out):
             nc.vector.quantize_mx(
                 v_codes[:].bitcast(E4M3),
                 v_scales[:],
-                v_half(q // 2)[:, q % 2, :, :].rearrange("p n j -> p (n j)"),
+                v_grouped[:, q * PIECE : (q + 1) * PIECE, :].rearrange("p n j -> p (n j)"),
             )
             score_passes(q, v_codes[:], v_scales[:], False)
             if q == 1:
-                weave(nc.vector.tensor_copy, 1, 2, v_late[:])
+                group_xm(nc.vector.tensor_copy, xm_early[0][:], xm_raw[0][:])
             for c, cut in enumerate(cuts[q]):
                 slopes[q, c] = tile("slopes%d_%d" % (q, c), [P, cut.stop - cut.start, PACK], F32)
                 nc.scalar.activation(
                     slopes[q, c][:], scores[q][:, :, cut].rearrange("p t n -> p n t"), ACT.Tanh, scale=-1.0
                 )
-        quantize_xm(0, xm_first[:])
+        quantize_xm(0, xm_early[0][:])
+        group_xm(nc.vector.tensor_copy, xm_early[1][:], xm_raw[1][:])
 
         g_codes, g_scales = mx_tiles("g", N)
         g_grouped = {}
@@ -184,7 +174,7 @@ def tile_attend_gds_lch_kernel(tc, xT, wT, vT, wt, xm, offs, out):
         staged = [tile("staged%d" % u, [P, N], F32) for u in range(D // P)]
 
         def gradient(u, first, end, bank):
-            grads = psum.tile([P, end - first], F32, name="grads%d_%d" % (u, first), tag="bank%d" % bank)
+            grads = psum.tile([P, end - first], F32, name="grads%d_%d" % (u, first), tag=bank)
             slots = slice(first, end)
             nc.tensor.matmul_mx(
                 grads[:],
@@ -205,32 +195,31 @@ def tile_attend_gds_lch_kernel(tc, xT, wT, vT, wt, xm, offs, out):
         weigh(1, 0)
         weigh(1, 1)
         quantize_g(0)
+        quantize_xm(1, xm_early[1][:], "slopes1_0")
         quantize_g(1)
-        xm_second = tile("xm_second", [P, P * PACK], BF16, "slopes1_0")
-        group_xm(nc.scalar.copy, xm_second[:], xm_raw[1][:, :, :P])
-        nc.scalar.copy(*gradient(0, 0, PIECE, 0))
-        nc.scalar.copy(*gradient(0, PIECE, HALF, 1))
+        nc.scalar.copy(*gradient(0, 0, PIECE, "bank0"))
+        nc.scalar.copy(*gradient(1, 0, PIECE, "bank1"))
+        nc.scalar.copy(*gradient(0, PIECE, HALF, "bank2"))
+        nc.scalar.copy(*gradient(1, PIECE, HALF, "bank3"))
         nc.scalar.activation(listed(windows[0][:], 0, HALF), staged[0][:, :HALF], ACT.Copy)
         weigh(2, 0)
         weigh(3, 0)
-        quantize_xm(1, xm_second[:])
-        nc.scalar.copy(*gradient(1, 0, HALF, 0))
         quantize_g(2)
         quantize_g(3)
-        late = [gradient(0, HALF, N, 2), gradient(1, HALF, N, 3)]
+        late = [gradient(0, HALF, N, "scores0"), gradient(1, HALF, N, "scores1")]
         xm_rest = tile("xm_rest", [P, 2 * P * PACK], BF16, "slopes3_0")
-        group_xm(nc.vector.tensor_copy, xm_rest[:], xm_raw[1][:, :, P:])
+        group_xm(nc.vector.tensor_copy, xm_rest[:], xm_raw[2][:])
         nc.vector.tensor_copy(*late[0])
         nc.vector.tensor_copy(*late[1])
         quantize_xm(2, xm_rest[:])
         nc.scalar.activation(listed(windows[0][:], HALF, N), staged[0][:, HALF:], ACT.Copy)
         store(0)
         nc.vector.tensor_copy(listed(windows[1][:], HALF, N), staged[1][:, HALF:])
-        nc.vector.tensor_copy(*gradient(3, HALF, N, 1))
+        nc.vector.tensor_copy(*gradient(3, HALF, N, "bank1"))
         nc.vector.tensor_copy(listed(windows[1][:], 0, HALF), staged[1][:, :HALF])
         store(1)
-        nc.scalar.copy(*gradient(2, 0, N, 2))
-        nc.scalar.copy(*gradient(3, 0, HALF, 3))
+        nc.scalar.copy(*gradient(2, 0, N, "scores0"))
+        nc.scalar.copy(*gradient(3, 0, HALF, "scores1"))
         nc.scalar.activation(listed(windows[2][:], 0, N), staged[2][:], ACT.Copy, scale=ones[:])
         store(2)
         nc.vector.tensor_copy(listed(windows[3][:], 0, N), staged[3][:])

from contextlib import ExitStack

import concourse.mybir as mybir

N, T, D, R = 512, 2048, 512, 512
FLOPS = 3 * 2 * R * D * N

F32 = mybir.dt.float32
BF16 = mybir.dt.bfloat16
U32 = mybir.dt.uint32
U16 = mybir.dt.uint16
U8 = mybir.dt.uint8
E4M3 = mybir.dt.float8_e4m3fn_x4
E5M2 = mybir.dt.float8_e5m2_x4
ACT = mybir.ActivationFunctionType
MULT = mybir.AluOpType.mult

P = 128
PACK = 4
HALF = N // 2
PIECES = 4
PIECE = N // PIECES


def tile_attend_gds_lch_kernel(tc, xT, wT, vT, wt, xm, offs, out):
    nc = tc.nc
    with ExitStack() as ctx:
        sb = ctx.enter_context(tc.tile_pool(name="sb", bufs=1))
        psum = ctx.enter_context(tc.psum_pool(name="psum", bufs=1))

        def tile(name, shape, dtype, tag=None):
            return sb.tile(shape, dtype, name=name, tag=tag or name, align_bytes=64)

        def mx_tiles(name, width, tag=None):
            return tile(name + "_codes", [P, width], U32, tag), tile(name + "_scales", [P, width], U8)

        def listed(window, first, end):
            return window.indirect(offsets[:, first // 16 : end // 16])

        offsets = sb.tile([P, N // 16], U16, name="offsets")
        row_weights = tile("row_weights", [P, PACK], F32)
        w_pairs = [tile("w_pair%d" % h, [P, 2, T], F32) for h in range(2)]
        w_rows = wT.rearrange("(p j) c -> p j c", j=PACK)
        nc.sync.dma_start(offsets[:], offs)
        nc.scalar.dma_start(w_pairs[0][:], w_rows[:, 0:2, :])
        nc.scalar.dma_start(row_weights[:], wt[0].rearrange("(p t) o -> p (t o)", t=PACK))
        nc.sync.dma_start(w_pairs[1][:], w_rows[:, 2:4, :])
        x_raw = tile("x_raw", [P, PACK, R], F32)
        nc.sync.dma_start(x_raw[:], xT[0].rearrange("(p j) r -> p j r", j=PACK))
        v_planes = [tile("v_plane%d" % j, [P, T], F32) for j in range(PACK)]
        v_rows = vT.rearrange("(p j) c -> p j c", j=PACK)
        for j in range(PACK):
            nc.sync.dma_start(v_planes[j][:], v_rows[:, j, :])
        xm_rows = xm[0].rearrange("(p t) d -> p t d", t=PACK)
        xm_raw = []
        for first, end in ((0, 1), (1, 2), (2, 4)):
            piece = tile("xm_raw%d" % first, [P, PACK, (end - first) * P], F32)
            nc.sync.dma_start(piece[:], xm_rows[:, :, first * P : end * P])
            xm_raw.append(piece)

        windows = [tile("window%d" % u, [P, T], F32) for u in range(D // P)]
        for window in windows:
            nc.gpsimd.memset(window[:], 0.0)
        ones = tile("ones", [P, 1], F32)
        nc.gpsimd.memset(ones[:], 1.0)

        w_picked = tile("w_picked", [P, PACK, N], F32)
        for j in range(2):
            nc.scalar.activation(w_picked[:, j, :], listed(w_pairs[0][:, j, :], 0, N), ACT.Copy)
            nc.vector.tensor_copy(w_picked[:, 2 + j, :], listed(w_pairs[1][:, j, :], 0, N))
        w_grouped = tile("w_grouped", [P, N * PACK], BF16)
        nc.scalar.activation(
            w_grouped[:].rearrange("p (c i j) -> p c j i", i=4, j=PACK),
            w_picked[:].rearrange("p j (c i) -> p c j i", i=4),
            ACT.Copy,
            scale=-1.0,
        )
        x_grouped = tile("x_grouped", [P, R * PACK], BF16)
        nc.vector.tensor_copy(
            x_grouped[:].rearrange("p (t m j) -> p m j t", t=PACK, j=PACK),
            x_raw[:].rearrange("p j (m t) -> p m j t", t=PACK),
        )
        x_rest = mx_tiles("x_rest", R - P)
        nc.vector.quantize_mx(x_rest[0][:].bitcast(E4M3), x_rest[1][:], x_grouped[:, P * PACK :])

        v_grouped = tile("v_grouped", [P, N, PACK], BF16)
        v_early = tile("v_early", [P, 2, N], BF16)
        nc.vector.tensor_copy(v_early[:, 0, :], listed(v_planes[0][:], 0, N))
        w_codes, w_scales = mx_tiles("w", N)
        nc.vector.quantize_mx(w_codes[:].bitcast(E4M3), w_scales[:], w_grouped[:])
        nc.vector.tensor_copy(v_early[:, 1, :], listed(v_planes[1][:], 0, N))
        x_first = mx_tiles("x_first", P, "v_plane1")
        nc.vector.quantize_mx(x_first[0][:].bitcast(E4M3), x_first[1][:], x_grouped[:, : P * PACK])
        nc.vector.tensor_copy(v_grouped[:, :, 0:2], v_early[:].rearrange("p j n -> p n j"))

        scores = [psum.tile([P, PACK, PIECE], F32, name="scores%d" % q, tag="scores%d" % q) for q in range(PIECES)]

        def score_passes(q, codes, scales, opens):
            for t in range(PACK):
                x_codes, x_scales = x_rest if t else x_first
                rows = slice((t - 1) * P, t * P) if t else slice(0, P)
                nc.tensor.matmul_mx(
                    scores[q][:, t, :],
                    lhsT=x_codes[:, rows].bitcast(E4M3),
                    lhsT_scale=x_scales[:, rows],
                    rhs=codes.bitcast(E4M3),
                    rhs_scale=scales,
                    start=(opens and t == 0),
                    stop=(not opens and t == PACK - 1),
                )

        for q in range(PIECES):
            slots = slice(q * PIECE, (q + 1) * PIECE)
            score_passes(q, w_codes[:, slots], w_scales[:, slots], True)

        nc.scalar.activation(v_grouped[:, :, 2], listed(v_planes[2][:], 0, N), ACT.Copy)
        for first in range(0, N, PIECE):
            end = first + PIECE
            nc.scalar.activation(v_grouped[:, first:end, 3], listed(v_planes[3][:], first, end), ACT.Copy)

        xm_mx = {}

        def group_xm(copy, grouped, raw):
            copy(
                grouped.rearrange("p (c i t) -> p c t i", i=4, t=PACK),
                raw.rearrange("p t (c i) -> p c t i", i=4),
            )

        def quantize_xm(first, grouped, tag=None):
            width = grouped.shape[1] // PACK
            codes, scales = mx_tiles("xm%d" % first, width, tag)
            nc.vector.quantize_mx(codes[:].bitcast(E4M3), scales[:], grouped)
            for u in range(width // P):
                xm_mx[first + u] = codes[:, u * P : (u + 1) * P], scales[:, u * P : (u + 1) * P]

        xm_early = [tile("xm_early%d" % u, [P, P * PACK], BF16) for u in range(2)]
        cuts = [[slice(0, PIECE // 2), slice(PIECE // 2, PIECE)]] * 2 + [[slice(0, PIECE)]] * 2
        slopes = {}
        for q in range(PIECES):
            v_codes, v_scales = mx_tiles("v%d" % q, PIECE)
            nc.vector.quantize_mx(
                v_codes[:].bitcast(E4M3),
                v_scales[:],
                v_grouped[:, q * PIECE : (q + 1) * PIECE, :].rearrange("p n j -> p (n j)"),
            )
            score_passes(q, v_codes[:], v_scales[:], False)
            if q == 1:
                group_xm(nc.vector.tensor_copy, xm_early[0][:], xm_raw[0][:])
            for c, cut in enumerate(cuts[q]):
                slopes[q, c] = tile("slopes%d_%d" % (q, c), [P, cut.stop - cut.start, PACK], F32)
                nc.scalar.activation(
                    slopes[q, c][:], scores[q][:, :, cut].rearrange("p t n -> p n t"), ACT.Tanh, scale=-1.0
                )
        quantize_xm(0, xm_early[0][:])
        group_xm(nc.vector.tensor_copy, xm_early[1][:], xm_raw[1][:])

        g_codes, g_scales = mx_tiles("g", N)
        g_grouped = {}

        def weigh(q, c):
            if c == 0:
                tag = "slopes1_1" if q == 2 else None
                g_grouped[q] = tile("g_grouped%d" % q, [P, PIECE, PACK], BF16, tag)
            cut = cuts[q][c]
            weights_wide = row_weights[:].unsqueeze(1).to_broadcast([P, cut.stop - cut.start, PACK])
            nc.vector.tensor_tensor(g_grouped[q][:, cut, :], slopes[q, c][:], weights_wide, MULT)

        def quantize_g(q):
            slots = slice(q * PIECE, (q + 1) * PIECE)
            nc.vector.quantize_mx(
                g_codes[:, slots].bitcast(E5M2), g_scales[:, slots], g_grouped[q][:].rearrange("p n t -> p (n t)")
            )

        staged = [tile("staged%d" % u, [P, N], F32) for u in range(D // P)]

        def gradient(u, first, end, bank):
            grads = psum.tile([P, end - first], F32, name="grads%d_%d" % (u, first), tag=bank)
            slots = slice(first, end)
            nc.tensor.matmul_mx(
                grads[:],
                lhsT=xm_mx[u][0].bitcast(E4M3),
                lhsT_scale=xm_mx[u][1],
                rhs=g_codes[:, slots].bitcast(E5M2),
                rhs_scale=g_scales[:, slots],
                start=True,
                stop=True,
            )
            return staged[u][:, slots], grads[:]

        def store(u):
            nc.sync.dma_start(out[u * P : (u + 1) * P, :], windows[u][:])

        weigh(0, 0)
        weigh(0, 1)
        weigh(1, 0)
        weigh(1, 1)
        quantize_g(0)
        quantize_xm(1, xm_early[1][:], "slopes1_0")
        quantize_g(1)
        nc.scalar.copy(*gradient(0, 0, PIECE, "bank0"))
        nc.scalar.copy(*gradient(1, 0, PIECE, "bank1"))
        nc.scalar.copy(*gradient(0, PIECE, HALF, "bank2"))
        nc.scalar.copy(*gradient(1, PIECE, HALF, "bank3"))
        nc.scalar.activation(listed(windows[0][:], 0, HALF), staged[0][:, :HALF], ACT.Copy)
        weigh(2, 0)
        weigh(3, 0)
        quantize_g(2)
        quantize_g(3)
        late = [gradient(0, HALF, N, "scores0"), gradient(1, HALF, N, "scores1")]
        xm_rest = tile("xm_rest", [P, 2 * P * PACK], BF16, "slopes3_0")
        group_xm(nc.vector.tensor_copy, xm_rest[:], xm_raw[2][:])
        nc.vector.tensor_copy(*late[0])
        nc.vector.tensor_copy(*late[1])
        quantize_xm(2, xm_rest[:])
        nc.scalar.activation(listed(windows[0][:], HALF, N), staged[0][:, HALF:], ACT.Copy)
        store(0)
        nc.vector.tensor_copy(listed(windows[1][:], HALF, N), staged[1][:, HALF:])
        nc.vector.tensor_copy(*gradient(3, HALF, N, "bank1"))
        nc.vector.tensor_copy(listed(windows[1][:], 0, HALF), staged[1][:, :HALF])
        store(1)
        nc.scalar.copy(*gradient(2, 0, N, "scores0"))
        nc.scalar.copy(*gradient(3, 0, HALF, "scores1"))
        nc.scalar.activation(listed(windows[2][:], 0, N), staged[2][:], ACT.Copy, scale=ones[:])
        store(2)
        nc.vector.tensor_copy(listed(windows[3][:], 0, N), staged[3][:])
        store(3)
